import numpy as np
import ml_dtypes


def mxq(x, axis, fmt="e4m3"):
    dtype, down = {"e4m3": (ml_dtypes.float8_e4m3fn, 7), "e5m2": (ml_dtypes.float8_e5m2, 14)}[fmt]
    v = np.moveaxis(np.asarray(x, np.float32).astype(ml_dtypes.bfloat16).astype(np.float64), axis, -1)
    blocks = v.reshape(v.shape[:-1] + (-1, 32))
    amax = np.abs(blocks).max(-1, keepdims=True)
    byte = np.maximum(np.where(amax > 0, np.frexp(amax)[1] - 1 + 127, 0) - down, 1)
    scale = np.exp2(byte - 127.0)
    codes = (blocks / scale).astype(np.float32).astype(dtype).astype(np.float64)
    return np.moveaxis((codes * scale).reshape(v.shape), -1, axis)


WIDE = False


def mx_kscale(k):
    if not WIDE:
        return np.ones(k)
    levels = np.array([10, -10, 5, -5, 0])
    if k % 512:
        return np.exp2(np.random.permutation(np.resize(levels, k // 32))).repeat(32)
    a = np.empty((k // 512, 16))
    for p in range(k // 512):
        a[p, :8] = np.random.permutation(np.resize(levels, 8))
        for g in range(8):
            far = levels[np.abs(levels - a[p, g]) >= 10]
            a[p, g + 8] = far[np.random.randint(len(far))]
    return np.exp2(a.ravel()).repeat(32)


def f64(x):
    return np.asarray(x).astype(np.float64)


def striped(idx):
    return np.tile(idx.reshape(-1, 16).T, (8, 1)).astype(np.uint16)


def unstriped(offs):
    return offs[:16].T.reshape(-1).astype(np.int64)


def pack_weight(w):
    k, n = w.shape
    w = f64(np.asarray(w, np.float32).astype(ml_dtypes.bfloat16)).reshape(k // 32, 32, n)
    amax = np.abs(w).max(1)
    byte = np.clip(np.where(amax > 0, np.frexp(amax)[1] - 1 + 127 - 7, 1), 1, 254)
    scaled = (w * np.exp2(127.0 - byte)[:, None, :]).reshape(k, n).astype(np.float32)
    words = np.ascontiguousarray(scaled.reshape(k // 512, 128, 4, n).transpose(0, 1, 3, 2)).astype(ml_dtypes.float8_e4m3fn).view(np.uint8)
    return words, np.ascontiguousarray(byte.astype(np.uint8).reshape(k // 512, 16, n))


def unpack_weight(words, scales):
    g, p, n, _ = words.shape
    vals = np.ascontiguousarray(words).view(ml_dtypes.float8_e4m3fn).astype(np.float64) * np.repeat(np.exp2(scales.astype(np.float64) - 127.0), 8, axis=1)[..., None]
    return vals.transpose(0, 1, 3, 2).reshape(g * 512, n)


K, T, S, H, D, W, U = 512, 1024, 512, 512, 4, 2048, 1024


def setup_inputs():
    n = np.random.standard_normal
    s = mx_kscale(K)[:, None]
    u = mx_kscale(H)
    packed_xT = pack_weight(n((K, T)) * s)
    packed_eT = pack_weight(n((H, W)) / np.sqrt(H) / u[:, None])
    return {
        "x_words": packed_xT[0],
        "x_scales": packed_xT[1],
        "w1": (n((K, H)) / np.sqrt(K) / s * u).astype(np.float32),
        "e_words": packed_eT[0],
        "e_scales": packed_eT[1],
        "offs": striped(np.random.permutation(T)[:S]),
        "sup": striped(np.random.permutation(W)[:U]),
    }


def reference(x_words, x_scales, w1, e_words, e_scales, offs, sup):
    xq = unpack_weight(x_words, x_scales)[:, unstriped(offs)]
    h = mxq(f64(w1), 0, "e4m3").T @ xq
    e_sup = unpack_weight(e_words, e_scales)[:, unstriped(sup)]
    y = mxq(h, 0, "e4m3").T @ e_sup
    ex = np.exp(y - y.max(axis=1, keepdims=True))
    p = ex / ex.sum(axis=1, keepdims=True)
    z = p.reshape(len(p), -1, D).sum(axis=2)
    return np.log(z + 1e-4)

@@ -1,0 +1,177 @@
+from contextlib import ExitStack
+
+import concourse.mybir as mybir
+
+K, T, S, H, D, W, U = 512, 1024, 512, 512, 4, 2048, 1024
+V = U // D
+FLOPS = 2 * K * H * S + 2 * H * S * U
+
+F32 = mybir.dt.float32
+BF16 = mybir.dt.bfloat16
+I32 = mybir.dt.int32
+U32 = mybir.dt.uint32
+U16 = mybir.dt.uint16
+U8 = mybir.dt.uint8
+FP8X4 = mybir.dt.float8_e4m3fn_x4
+ACT = mybir.ActivationFunctionType
+ALU = mybir.AluOpType
+AX = mybir.AxisListType
+
+P = 128
+PACK = 4
+TILES = S // P
+HALVES = 2
+HALF = U // HALVES
+VH = V // HALVES
+LIST_ROWS = 16
+EPS = 1e-4
+
+
+def load_scale_rows(nc, table, scales):
+    for q in range(4):
+        nc.sync.dma_start(
+            out=table[32 * q : 32 * q + 4, :].bitcast(I32),
+            in_=scales[0, 4 * q : 4 * q + 4, :].bitcast(I32),
+        )
+
+
+def load_words(nc, table, words):
+    nc.sync.dma_start(out=table[:].bitcast(I32), in_=words[0].rearrange("p n t -> p (n t)").bitcast(I32))
+
+
+def tile_picked_ymatch_log_p_kernel(tc, x_words, x_scales, w1, e_words, e_scales, offs, sup, out):
+    nc = tc.nc
+    with ExitStack() as ctx:
+        keep = ctx.enter_context(tc.tile_pool(name="keep", bufs=1))
+        psum = ctx.enter_context(tc.psum_pool(name="psum", bufs=8))
+
+        offs_sb = keep.tile([P, S // LIST_ROWS], U16, name="offs_sb")
+        sup_sb = keep.tile([P, U // LIST_ROWS], U16, name="sup_sb")
+        xw_table = keep.tile([P, T], U32, name="xw_table", align_bytes=64)
+        xs_table = keep.tile([P, T], U8, name="xs_table", align_bytes=64)
+        ew_table = keep.tile([P, W], U32, name="ew_table", align_bytes=64)
+        es_table = keep.tile([P, W], U8, name="es_table", align_bytes=64)
+        w_raw = [keep.tile([P, PACK, H // 2], F32, name=f"w_raw{a}") for a in range(2)]
+
+        nc.vector.memset(xs_table[:].bitcast(I32), 0)
+        nc.vector.memset(es_table[:].bitcast(I32), 0)
+
+        nc.sync.dma_start(offs_sb[:], offs)
+        load_words(nc, xw_table, x_words)
+        load_scale_rows(nc, xs_table, x_scales)
+        w_rows = w1.rearrange("(p j) c -> p j c", j=PACK)
+        for a in range(2):
+            nc.sync.dma_start(out=w_raw[a][:], in_=w_rows[:, :, a * (H // 2) : (a + 1) * (H // 2)])
+        nc.sync.dma_start(sup_sb[:], sup)
+        load_scale_rows(nc, es_table, e_scales)
+        load_words(nc, ew_table, e_words)
+
+        x_codes = keep.tile([P, S], U32, name="x_codes", align_bytes=64)
+        x_scale = keep.tile([P, S], U8, name="x_scale", align_bytes=64)
+        nc.vector.tensor_copy(x_codes[:], xw_table[:].indirect(offs_sb[:]))
+        nc.vector.tensor_copy(x_scale[:], xs_table[:].indirect(offs_sb[:]))
+
+        w_bf = keep.tile([P, PACK * H], BF16, name="w_bf", align_bytes=64)
+        w_view = w_bf[:].rearrange("p (t m j) -> p m t j", t=PACK, j=PACK)
+        for a in range(2):
+            nc.scalar.activation(
+                out=w_view[:, a * (P // 2) : (a + 1) * (P // 2)],
+                in_=w_raw[a][:].rearrange("p j (m t) -> p m t j", t=PACK),
+                func=ACT.Copy,
+            )
+        w_codes = keep.tile([P, H], U32, name="w_codes", align_bytes=64)
+        w_scale = keep.tile([P, H], U8, name="w_scale", align_bytes=64)
+        nc.vector.quantize_mx(out=w_codes[:].bitcast(FP8X4), scales=w_scale[:], in_=w_bf[:])
+
+        list_cols = HALF // LIST_ROWS
+        e_scale = []
+        for a in range(HALVES):
+            es = keep.tile([P, HALF], U8, name=f"e_scale{a}", align_bytes=64)
+            nc.vector.tensor_copy(es[:], es_table[:].indirect(sup_sb[:, a * list_cols : (a + 1) * list_cols]))
+            e_scale.append(es)
+
+        h_codes, h_scale = [], []
+        for i in range(TILES):
+            tok = slice(i * P, (i + 1) * P)
+            bank = psum.tile([P, PACK * P], F32, name="bank")
+            for t in range(PACK):
+                nc.tensor.matmul_mx(
+                    out=bank[:, t * P : (t + 1) * P],
+                    lhsT=w_codes[:, t * P : (t + 1) * P].bitcast(FP8X4),
+                    lhsT_scale=w_scale[:, t * P : (t + 1) * P],
+                    rhs=x_codes[:, tok].bitcast(FP8X4),
+                    rhs_scale=x_scale[:, tok],
+                    start=True,
+                    stop=True,
+                )
+            h_bf = keep.tile([P, P * PACK], BF16, name=f"h_bf{i}", align_bytes=64)
+            nc.scalar.copy(
+                out=h_bf[:].rearrange("p (n t) -> p n t", t=PACK),
+                in_=bank[:].rearrange("p (t n) -> p n t", t=PACK),
+            )
+            hc = keep.tile([P, P], U32, name=f"h_codes{i}", align_bytes=64)
+            hs = keep.tile([P, P], U8, name=f"h_scale{i}", align_bytes=64)
+            nc.vector.quantize_mx(out=hc[:].bitcast(FP8X4), scales=hs[:], in_=h_bf[:])
+            h_codes.append(hc)
+            h_scale.append(hs)
+
+        e_codes = []
+        for a in range(HALVES):
+            ec = keep.tile([P, HALF], U32, name=f"e_codes{a}", align_bytes=64)
+            nc.vector.tensor_copy(ec[:], ew_table[:].indirect(sup_sb[:, a * list_cols : (a + 1) * list_cols]))
+            e_codes.append(ec)
+
+        neg_max = keep.tile([P, TILES, HALVES], F32, name="neg_max")
+        half_sum = keep.tile([P, TILES, HALVES], F32, name="half_sum")
+        ex = [keep.tile([P, D, V], F32, name=f"ex{i}") for i in range(TILES)]
+        for i in range(TILES):
+            for a in range(HALVES):
+                bank = psum.tile([P, HALF], F32, name="bank")
+                nc.tensor.matmul_mx(
+                    out=bank[:],
+                    lhsT=h_codes[i][:].bitcast(FP8X4),
+                    lhsT_scale=h_scale[i][:],
+                    rhs=e_codes[a][:].bitcast(FP8X4),
+                    rhs_scale=e_scale[a][:],
+                    start=True,
+                    stop=True,
+                )
+                nc.vector.tensor_reduce(out=neg_max[:, i, a : a + 1], in_=bank[:], axis=AX.X, op=ALU.max, negate=True)
+                nc.scalar.activation(
+                    out=ex[i][:, :, a * VH : (a + 1) * VH],
+                    in_=bank[:].rearrange("p (v d) -> p d v", d=D),
+                    func=ACT.Exp,
+                    bias=neg_max[:, i, a : a + 1],
+                    accum_out=half_sum[:, i, a : a + 1],
+                )
+
+        neg_row_max = keep.tile([P, TILES], F32, name="neg_row_max")
+        gap = keep.tile([P, TILES, HALVES], F32, name="gap")
+        factor = keep.tile([P, TILES, HALVES], F32, name="factor")
+        scaled_sum = keep.tile([P, TILES, HALVES], F32, name="scaled_sum")
+        row_sum = keep.tile([P, TILES], F32, name="row_sum")
+        inv_sum = keep.tile([P, TILES], F32, name="inv_sum")
+        weight = keep.tile([P, TILES, HALVES], F32, name="weight")
+        nc.vector.tensor_reduce(out=neg_row_max[:], in_=neg_max[:], axis=AX.X, op=ALU.min)
+        nc.vector.tensor_tensor(
+            out=gap[:], in0=neg_row_max[:].unsqueeze(2).to_broadcast([P, TILES, HALVES]), in1=neg_max[:], op=ALU.subtract
+        )
+        nc.scalar.activation(out=factor[:], in_=gap[:], func=ACT.Exp)
+        nc.vector.tensor_tensor(out=scaled_sum[:], in0=factor[:], in1=half_sum[:], op=ALU.mult)
+        nc.vector.tensor_reduce(out=row_sum[:], in_=scaled_sum[:], axis=AX.X, op=ALU.add)
+        nc.vector.reciprocal(out=inv_sum[:], in_=row_sum[:])
+        nc.vector.tensor_tensor(
+            out=weight[:], in0=factor[:], in1=inv_sum[:].unsqueeze(2).to_broadcast([P, TILES, HALVES]), op=ALU.mult
+        )
+
+        for i in range(TILES):
+            pair = keep.tile([P, 2, V], F32, name=f"pair{i}")
+            z = keep.tile([P, V], F32, name=f"z{i}")
+            res = keep.tile([P, V], F32, name=f"res{i}")
+            adder = nc.gpsimd if i < 2 else nc.vector
+            adder.tensor_tensor(out=pair[:], in0=ex[i][:, 0:2, :], in1=ex[i][:, 2:4, :], op=ALU.add)
+            nc.vector.tensor_tensor(out=z[:], in0=pair[:, 0, :], in1=pair[:, 1, :], op=ALU.add)
+            for a in range(HALVES):
+                cols = slice(a * VH, (a + 1) * VH)
+                nc.scalar.activation(out=res[:, cols], in_=z[:, cols], func=ACT.Ln, scale=weight[:, i, a : a + 1], bias=EPS)
+            nc.sync.dma_start(out=out[i * P : (i + 1) * P, :], in_=res[:])

@@ -25,6 +25,7 @@ HALF = U // HALVES
 VH = V // HALVES
 LIST_ROWS = 16
 EPS = 1e-4
+MAX_GAP = 64.0
 
 
 def load_scale_rows(nc, table, scales):
@@ -56,14 +57,14 @@ def tile_picked_ymatch_log_p_kernel(tc, x_words, x_scales, w1, e_words, e_scales
         nc.vector.memset(xs_table[:].bitcast(I32), 0)
         nc.vector.memset(es_table[:].bitcast(I32), 0)
 
+        w_rows = w1.rearrange("(p j) c -> p j c", j=PACK)
         nc.sync.dma_start(offs_sb[:], offs)
         load_words(nc, xw_table, x_words)
         load_scale_rows(nc, xs_table, x_scales)
-        w_rows = w1.rearrange("(p j) c -> p j c", j=PACK)
-        for a in range(2):
-            nc.sync.dma_start(out=w_raw[a][:], in_=w_rows[:, :, a * (H // 2) : (a + 1) * (H // 2)])
+        nc.sync.dma_start(out=w_raw[0][:], in_=w_rows[:, :, 0 : H // 2])
         nc.sync.dma_start(sup_sb[:], sup)
         load_scale_rows(nc, es_table, e_scales)
+        nc.sync.dma_start(out=w_raw[1][:], in_=w_rows[:, :, H // 2 : H])
         load_words(nc, ew_table, e_words)
 
         x_codes = keep.tile([P, S], U32, name="x_codes", align_bytes=64)
@@ -123,7 +124,7 @@ def tile_picked_ymatch_log_p_kernel(tc, x_words, x_scales, w1, e_words, e_scales
 
         neg_max = keep.tile([P, TILES, HALVES], F32, name="neg_max")
         half_sum = keep.tile([P, TILES, HALVES], F32, name="half_sum")
-        ex = [keep.tile([P, D, V], F32, name=f"ex{i}") for i in range(TILES)]
+        ex = [keep.tile([P, HALVES, D, VH], F32, name=f"ex{i}") for i in range(TILES)]
         for i in range(TILES):
             for a in range(HALVES):
                 bank = psum.tile([P, HALF], F32, name="bank")
@@ -138,39 +139,33 @@ def tile_picked_ymatch_log_p_kernel(tc, x_words, x_scales, w1, e_words, e_scales
                 )
                 nc.vector.tensor_reduce(out=neg_max[:, i, a : a + 1], in_=bank[:], axis=AX.X, op=ALU.max, negate=True)
                 nc.scalar.activation(
-                    out=ex[i][:, :, a * VH : (a + 1) * VH],
+                    out=ex[i][:, a],
                     in_=bank[:].rearrange("p (v d) -> p d v", d=D),
                     func=ACT.Exp,
                     bias=neg_max[:, i, a : a + 1],
                     accum_out=half_sum[:, i, a : a + 1],
                 )
 
-        neg_row_max = keep.tile([P, TILES], F32, name="neg_row_max")
         gap = keep.tile([P, TILES, HALVES], F32, name="gap")
-        factor = keep.tile([P, TILES, HALVES], F32, name="factor")
-        scaled_sum = keep.tile([P, TILES, HALVES], F32, name="scaled_sum")
-        row_sum = keep.tile([P, TILES], F32, name="row_sum")
-        inv_sum = keep.tile([P, TILES], F32, name="inv_sum")
+        clamped = keep.tile([P, TILES, HALVES], F32, name="clamped")
+        factor = keep.tile([P, TILES, HALVES], F32, name="factor", tag="after_factor")
+        other = keep.tile([P, TILES, HALVES], F32, name="other")
+        total = keep.tile([P, TILES, HALVES], F32, name="total", tag="after_total")
         weight = keep.tile([P, TILES, HALVES], F32, name="weight")
-        nc.vector.tensor_reduce(out=neg_row_max[:], in_=neg_max[:], axis=AX.X, op=ALU.min)
-        nc.vector.tensor_tensor(
-            out=gap[:], in0=neg_row_max[:].unsqueeze(2).to_broadcast([P, TILES, HALVES]), in1=neg_max[:], op=ALU.subtract
-        )
-        nc.scalar.activation(out=factor[:], in_=gap[:], func=ACT.Exp)
-        nc.vector.tensor_tensor(out=scaled_sum[:], in0=factor[:], in1=half_sum[:], op=ALU.mult)
-        nc.vector.tensor_reduce(out=row_sum[:], in_=scaled_sum[:], axis=AX.X, op=ALU.add)
-        nc.vector.reciprocal(out=inv_sum[:], in_=row_sum[:])
-        nc.vector.tensor_tensor(
-            out=weight[:], in0=factor[:], in1=inv_sum[:].unsqueeze(2).to_broadcast([P, TILES, HALVES]), op=ALU.mult
-        )
+        nc.vector.tensor_tensor(out=gap[:], in0=neg_max[:], in1=neg_max[:, :, ::-1], op=ALU.subtract)
+        nc.vector.tensor_scalar_min(out=clamped[:], in0=gap[:], scalar1=MAX_GAP)
+        nc.scalar.activation(out=factor[:], in_=clamped[:], func=ACT.Exp)
+        nc.vector.tensor_tensor(out=other[:], in0=factor[:], in1=half_sum[:, :, ::-1], op=ALU.mult)
+        nc.vector.tensor_tensor(out=total[:], in0=other[:], in1=half_sum[:], op=ALU.add)
+        nc.vector.reciprocal(out=weight[:], in_=total[:])
 
         for i in range(TILES):
-            pair = keep.tile([P, 2, V], F32, name=f"pair{i}")
-            z = keep.tile([P, V], F32, name=f"z{i}")
+            pair = keep.tile([P, HALVES, 2, VH], F32, name=f"pair{i}", tag="after_total" if i == 3 else f"pair{i}")
+            z = keep.tile([P, V], F32, name=f"z{i}", tag="after_factor" if i == 2 else f"z{i}")
             res = keep.tile([P, V], F32, name=f"res{i}")
             adder = nc.gpsimd if i < 2 else nc.vector
-            adder.tensor_tensor(out=pair[:], in0=ex[i][:, 0:2, :], in1=ex[i][:, 2:4, :], op=ALU.add)
-            nc.vector.tensor_tensor(out=z[:], in0=pair[:, 0, :], in1=pair[:, 1, :], op=ALU.add)
+            adder.tensor_tensor(out=pair[:], in0=ex[i][:, :, 0:2, :], in1=ex[i][:, :, 2:4, :], op=ALU.add)
+            nc.vector.tensor_tensor(out=z[:].rearrange("p (a v) -> p a v", a=HALVES), in0=pair[:, :, 0, :], in1=pair[:, :, 1, :], op=ALU.add)
             for a in range(HALVES):
                 cols = slice(a * VH, (a + 1) * VH)
                 nc.scalar.activation(out=res[:, cols], in_=z[:, cols], func=ACT.Ln, scale=weight[:, i, a : a + 1], bias=EPS)

@@ -26,6 +26,7 @@ VH = V // HALVES
 LIST_ROWS = 16
 EPS = 1e-4
 MAX_GAP = 64.0
+W_SPLIT = 384
 
 
 def load_scale_rows(nc, table, scales):
@@ -52,7 +53,8 @@ def tile_picked_ymatch_log_p_kernel(tc, x_words, x_scales, w1, e_words, e_scales
         xs_table = keep.tile([P, T], U8, name="xs_table", align_bytes=64)
         ew_table = keep.tile([P, W], U32, name="ew_table", align_bytes=64)
         es_table = keep.tile([P, W], U8, name="es_table", align_bytes=64)
-        w_raw = [keep.tile([P, PACK, H // 2], F32, name=f"w_raw{a}") for a in range(2)]
+        w_cols = [slice(0, W_SPLIT), slice(W_SPLIT, H)]
+        w_raw = [keep.tile([P, PACK, c.stop - c.start], F32, name=f"w_raw{a}") for a, c in enumerate(w_cols)]
 
         nc.vector.memset(xs_table[:].bitcast(I32), 0)
         nc.vector.memset(es_table[:].bitcast(I32), 0)
@@ -61,10 +63,10 @@ def tile_picked_ymatch_log_p_kernel(tc, x_words, x_scales, w1, e_words, e_scales
         nc.sync.dma_start(offs_sb[:], offs)
         load_words(nc, xw_table, x_words)
         load_scale_rows(nc, xs_table, x_scales)
-        nc.sync.dma_start(out=w_raw[0][:], in_=w_rows[:, :, 0 : H // 2])
         nc.sync.dma_start(sup_sb[:], sup)
+        nc.sync.dma_start(out=w_raw[0][:], in_=w_rows[:, :, w_cols[0]])
         load_scale_rows(nc, es_table, e_scales)
-        nc.sync.dma_start(out=w_raw[1][:], in_=w_rows[:, :, H // 2 : H])
+        nc.sync.dma_start(out=w_raw[1][:], in_=w_rows[:, :, w_cols[1]])
         load_words(nc, ew_table, e_words)
 
         x_codes = keep.tile([P, S], U32, name="x_codes", align_bytes=64)
@@ -74,9 +76,9 @@ def tile_picked_ymatch_log_p_kernel(tc, x_words, x_scales, w1, e_words, e_scales
 
         w_bf = keep.tile([P, PACK * H], BF16, name="w_bf", align_bytes=64)
         w_view = w_bf[:].rearrange("p (t m j) -> p m t j", t=PACK, j=PACK)
-        for a in range(2):
+        for a, c in enumerate(w_cols):
             nc.scalar.activation(
-                out=w_view[:, a * (P // 2) : (a + 1) * (P // 2)],
+                out=w_view[:, c.start // PACK : c.stop // PACK],
                 in_=w_raw[a][:].rearrange("p j (m t) -> p m t j", t=PACK),
                 func=ACT.Copy,
             )
@@ -119,7 +121,12 @@ def tile_picked_ymatch_log_p_kernel(tc, x_words, x_scales, w1, e_words, e_scales
         e_codes = []
         for a in range(HALVES):
             ec = keep.tile([P, HALF], U32, name=f"e_codes{a}", align_bytes=64)
-            nc.vector.tensor_copy(ec[:], ew_table[:].indirect(sup_sb[:, a * list_cols : (a + 1) * list_cols]))
+            pieces = a + 1
+            for b in range(pieces):
+                lo = b * HALF // pieces
+                hi = (b + 1) * HALF // pieces
+                entries = sup_sb[:, (a * HALF + lo) // LIST_ROWS : (a * HALF + hi) // LIST_ROWS]
+                nc.vector.tensor_copy(ec[:, lo:hi], ew_table[:].indirect(entries))
             e_codes.append(ec)
 
         neg_max = keep.tile([P, TILES, HALVES], F32, name="neg_max")
@@ -150,7 +157,7 @@ def tile_picked_ymatch_log_p_kernel(tc, x_words, x_scales, w1, e_words, e_scales
         clamped = keep.tile([P, TILES, HALVES], F32, name="clamped")
         factor = keep.tile([P, TILES, HALVES], F32, name="factor", tag="after_factor")
         other = keep.tile([P, TILES, HALVES], F32, name="other")
-        total = keep.tile([P, TILES, HALVES], F32, name="total", tag="after_total")
+        total = keep.tile([P, TILES, HALVES], F32, name="total")
         weight = keep.tile([P, TILES, HALVES], F32, name="weight")
         nc.vector.tensor_tensor(out=gap[:], in0=neg_max[:], in1=neg_max[:, :, ::-1], op=ALU.subtract)
         nc.vector.tensor_scalar_min(out=clamped[:], in0=gap[:], scalar1=MAX_GAP)
@@ -160,11 +167,14 @@ def tile_picked_ymatch_log_p_kernel(tc, x_words, x_scales, w1, e_words, e_scales
         nc.vector.reciprocal(out=weight[:], in_=total[:])
 
         for i in range(TILES):
-            pair = keep.tile([P, HALVES, 2, VH], F32, name=f"pair{i}", tag="after_total" if i == 3 else f"pair{i}")
+            pair = keep.tile([P, HALVES, 2, VH], F32, name=f"pair{i}")
             z = keep.tile([P, V], F32, name=f"z{i}", tag="after_factor" if i == 2 else f"z{i}")
             res = keep.tile([P, V], F32, name=f"res{i}")
-            adder = nc.gpsimd if i < 2 else nc.vector
-            adder.tensor_tensor(out=pair[:], in0=ex[i][:, :, 0:2, :], in1=ex[i][:, :, 2:4, :], op=ALU.add)
+            if i < 2:
+                for a in range(HALVES):
+                    nc.gpsimd.tensor_tensor(out=pair[:, a], in0=ex[i][:, a, 0:2, :], in1=ex[i][:, a, 2:4, :], op=ALU.add)
+            else:
+                nc.vector.tensor_tensor(out=pair[:], in0=ex[i][:, :, 0:2, :], in1=ex[i][:, :, 2:4, :], op=ALU.add)
             nc.vector.tensor_tensor(out=z[:].rearrange("p (a v) -> p a v", a=HALVES), in0=pair[:, :, 0, :], in1=pair[:, :, 1, :], op=ALU.add)
             for a in range(HALVES):
                 cols = slice(a * VH, (a + 1) * VH)

@@ -131,7 +131,7 @@ def tile_picked_ymatch_log_p_kernel(tc, x_words, x_scales, w1, e_words, e_scales
 
         neg_max = keep.tile([P, TILES, HALVES], F32, name="neg_max")
         half_sum = keep.tile([P, TILES, HALVES], F32, name="half_sum")
-        ex = [keep.tile([P, HALVES, D, VH], F32, name=f"ex{i}") for i in range(TILES)]
+        ex = [keep.tile([P, U], F32, name=f"ex{i}") for i in range(TILES)]
         for i in range(TILES):
             for a in range(HALVES):
                 bank = psum.tile([P, HALF], F32, name="bank")
@@ -146,8 +146,8 @@ def tile_picked_ymatch_log_p_kernel(tc, x_words, x_scales, w1, e_words, e_scales
                 )
                 nc.vector.tensor_reduce(out=neg_max[:, i, a : a + 1], in_=bank[:], axis=AX.X, op=ALU.max, negate=True)
                 nc.scalar.activation(
-                    out=ex[i][:, a],
-                    in_=bank[:].rearrange("p (v d) -> p d v", d=D),
+                    out=ex[i][:, a * HALF : (a + 1) * HALF],
+                    in_=bank[:],
                     func=ACT.Exp,
                     bias=neg_max[:, i, a : a + 1],
                     accum_out=half_sum[:, i, a : a + 1],
@@ -167,15 +167,16 @@ def tile_picked_ymatch_log_p_kernel(tc, x_words, x_scales, w1, e_words, e_scales
         nc.vector.reciprocal(out=weight[:], in_=total[:])
 
         for i in range(TILES):
-            pair = keep.tile([P, HALVES, 2, VH], F32, name=f"pair{i}")
+            pair = keep.tile([P, U // 2], F32, name=f"pair{i}")
             z = keep.tile([P, V], F32, name=f"z{i}", tag="after_factor" if i == 2 else f"z{i}")
             res = keep.tile([P, V], F32, name=f"res{i}")
             if i < 2:
                 for a in range(HALVES):
-                    nc.gpsimd.tensor_tensor(out=pair[:, a], in0=ex[i][:, a, 0:2, :], in1=ex[i][:, a, 2:4, :], op=ALU.add)
+                    lo, hi = a * HALF, (a + 1) * HALF
+                    nc.gpsimd.tensor_tensor(out=pair[:, lo // 2 : hi // 2], in0=ex[i][:, lo:hi:2], in1=ex[i][:, lo + 1 : hi : 2], op=ALU.add)
             else:
-                nc.vector.tensor_tensor(out=pair[:], in0=ex[i][:, :, 0:2, :], in1=ex[i][:, :, 2:4, :], op=ALU.add)
-            nc.vector.tensor_tensor(out=z[:].rearrange("p (a v) -> p a v", a=HALVES), in0=pair[:, :, 0, :], in1=pair[:, :, 1, :], op=ALU.add)
+                nc.vector.tensor_tensor(out=pair[:], in0=ex[i][:, 0::2], in1=ex[i][:, 1::2], op=ALU.add)
+            nc.vector.tensor_tensor(out=z[:], in0=pair[:, 0::2], in1=pair[:, 1::2], op=ALU.add)
             for a in range(HALVES):
                 cols = slice(a * VH, (a + 1) * VH)
                 nc.scalar.activation(out=res[:, cols], in_=z[:, cols], func=ACT.Ln, scale=weight[:, i, a : a + 1], bias=EPS)

@@ -1,6 +1,7 @@
 from contextlib import ExitStack
 
 import concourse.mybir as mybir
+from concourse.masks import make_identity
 
 K, T, S, H, D, W, U = 512, 1024, 512, 512, 4, 2048, 1024
 V = U // D
@@ -27,12 +28,14 @@ LIST_ROWS = 16
 EPS = 1e-4
 MAX_GAP = 64.0
 W_SPLIT = 384
+E_ROW = 0
+PE_TILES = 3
 
 
-def load_scale_rows(nc, table, scales):
+def load_scale_rows(nc, table, scales, row):
     for q in range(4):
         nc.sync.dma_start(
-            out=table[32 * q : 32 * q + 4, :].bitcast(I32),
+            out=table[32 * q + row : 32 * q + row + 4, :].bitcast(I32),
             in_=scales[0, 4 * q : 4 * q + 4, :].bitcast(I32),
         )
 
@@ -41,11 +44,15 @@ def load_words(nc, table, words):
     nc.sync.dma_start(out=table[:].bitcast(I32), in_=words[0].rearrange("p n t -> p (n t)").bitcast(I32))
 
 
+def y_tag(i, a):
+    return f"bank{(TILES + HALVES * i + a) % 8}"
+
+
 def tile_picked_ymatch_log_p_kernel(tc, x_words, x_scales, w1, e_words, e_scales, offs, sup, out):
     nc = tc.nc
     with ExitStack() as ctx:
         keep = ctx.enter_context(tc.tile_pool(name="keep", bufs=1))
-        psum = ctx.enter_context(tc.psum_pool(name="psum", bufs=8))
+        psum = ctx.enter_context(tc.psum_pool(name="psum", bufs=1))
 
         offs_sb = keep.tile([P, S // LIST_ROWS], U16, name="offs_sb")
         sup_sb = keep.tile([P, U // LIST_ROWS], U16, name="sup_sb")
@@ -56,16 +63,18 @@ def tile_picked_ymatch_log_p_kernel(tc, x_words, x_scales, w1, e_words, e_scales
         w_cols = [slice(0, W_SPLIT), slice(W_SPLIT, H)]
         w_raw = [keep.tile([P, PACK, c.stop - c.start], F32, name=f"w_raw{a}") for a, c in enumerate(w_cols)]
 
+        ident = keep.tile([P, P], F32, name="ident")
         nc.vector.memset(xs_table[:].bitcast(I32), 0)
         nc.vector.memset(es_table[:].bitcast(I32), 0)
+        make_identity(nc, ident[:])
 
         w_rows = w1.rearrange("(p j) c -> p j c", j=PACK)
         nc.sync.dma_start(offs_sb[:], offs)
         load_words(nc, xw_table, x_words)
-        load_scale_rows(nc, xs_table, x_scales)
+        load_scale_rows(nc, xs_table, x_scales, 0)
         nc.sync.dma_start(sup_sb[:], sup)
         nc.sync.dma_start(out=w_raw[0][:], in_=w_rows[:, :, w_cols[0]])
-        load_scale_rows(nc, es_table, e_scales)
+        load_scale_rows(nc, es_table, e_scales, E_ROW)
         nc.sync.dma_start(out=w_raw[1][:], in_=w_rows[:, :, w_cols[1]])
         load_words(nc, ew_table, e_words)
 
@@ -96,7 +105,7 @@ def tile_picked_ymatch_log_p_kernel(tc, x_words, x_scales, w1, e_words, e_scales
         h_codes, h_scale = [], []
         for i in range(TILES):
             tok = slice(i * P, (i + 1) * P)
-            bank = psum.tile([P, PACK * P], F32, name="bank")
+            bank = psum.tile([P, PACK * P], F32, name=f"h_bank{i}", tag=f"bank{i}")
             for t in range(PACK):
                 nc.tensor.matmul_mx(
                     out=bank[:, t * P : (t + 1) * P],
@@ -131,23 +140,23 @@ def tile_picked_ymatch_log_p_kernel(tc, x_words, x_scales, w1, e_words, e_scales
 
         neg_max = keep.tile([P, TILES, HALVES], F32, name="neg_max")
         half_sum = keep.tile([P, TILES, HALVES], F32, name="half_sum")
-        ex = [keep.tile([P, U], F32, name=f"ex{i}") for i in range(TILES)]
+        ex = [keep.tile([P, HALVES, D, VH], F32, name=f"ex{i}") for i in range(TILES)]
         for i in range(TILES):
             for a in range(HALVES):
-                bank = psum.tile([P, HALF], F32, name="bank")
+                bank = psum.tile([P, HALF], F32, name=f"y_bank{i}{a}", tag=y_tag(i, a))
                 nc.tensor.matmul_mx(
                     out=bank[:],
                     lhsT=h_codes[i][:].bitcast(FP8X4),
                     lhsT_scale=h_scale[i][:],
                     rhs=e_codes[a][:].bitcast(FP8X4),
-                    rhs_scale=e_scale[a][:],
+                    rhs_scale=e_scale[a][E_ROW:P, :],
                     start=True,
                     stop=True,
                 )
                 nc.vector.tensor_reduce(out=neg_max[:, i, a : a + 1], in_=bank[:], axis=AX.X, op=ALU.max, negate=True)
                 nc.scalar.activation(
-                    out=ex[i][:, a * HALF : (a + 1) * HALF],
-                    in_=bank[:],
+                    out=ex[i][:, a],
+                    in_=bank[:].rearrange("p (v d) -> p d v", d=D),
                     func=ACT.Exp,
                     bias=neg_max[:, i, a : a + 1],
                     accum_out=half_sum[:, i, a : a + 1],
@@ -155,7 +164,7 @@ def tile_picked_ymatch_log_p_kernel(tc, x_words, x_scales, w1, e_words, e_scales
 
         gap = keep.tile([P, TILES, HALVES], F32, name="gap")
         clamped = keep.tile([P, TILES, HALVES], F32, name="clamped")
-        factor = keep.tile([P, TILES, HALVES], F32, name="factor", tag="after_factor")
+        factor = keep.tile([P, TILES, HALVES], F32, name="factor")
         other = keep.tile([P, TILES, HALVES], F32, name="other")
         total = keep.tile([P, TILES, HALVES], F32, name="total")
         weight = keep.tile([P, TILES, HALVES], F32, name="weight")
@@ -166,18 +175,29 @@ def tile_picked_ymatch_log_p_kernel(tc, x_words, x_scales, w1, e_words, e_scales
         nc.vector.tensor_tensor(out=total[:], in0=other[:], in1=half_sum[:], op=ALU.add)
         nc.vector.reciprocal(out=weight[:], in_=total[:])
 
-        for i in range(TILES):
-            pair = keep.tile([P, U // 2], F32, name=f"pair{i}")
-            z = keep.tile([P, V], F32, name=f"z{i}", tag="after_factor" if i == 2 else f"z{i}")
-            res = keep.tile([P, V], F32, name=f"res{i}")
-            if i < 2:
-                for a in range(HALVES):
-                    lo, hi = a * HALF, (a + 1) * HALF
-                    nc.gpsimd.tensor_tensor(out=pair[:, lo // 2 : hi // 2], in0=ex[i][:, lo:hi:2], in1=ex[i][:, lo + 1 : hi : 2], op=ALU.add)
-            else:
-                nc.vector.tensor_tensor(out=pair[:], in0=ex[i][:, 0::2], in1=ex[i][:, 1::2], op=ALU.add)
-            nc.vector.tensor_tensor(out=z[:], in0=pair[:, 0::2], in1=pair[:, 1::2], op=ALU.add)
+        z = []
+        for i in range(PE_TILES):
+            turned = psum.tile([P, HALVES, P], F32, name=f"turned{i}", tag=y_tag(i, 0))
             for a in range(HALVES):
-                cols = slice(a * VH, (a + 1) * VH)
-                nc.scalar.activation(out=res[:, cols], in_=z[:, cols], func=ACT.Ln, scale=weight[:, i, a : a + 1], bias=EPS)
-            nc.sync.dma_start(out=out[i * P : (i + 1) * P, :], in_=res[:])
+                for d in range(D):
+                    nc.tensor.matmul(
+                        turned[:, a, :], lhsT=ex[i][:, a, d, :], rhs=ident[:], is_transpose=True, start=d == 0, stop=d == D - 1
+                    )
+            turned_sb = keep.tile([P, HALVES, P], F32, name=f"turned_sb{i}")
+            nc.vector.tensor_copy(turned_sb[:], turned[:])
+            back = psum.tile([P, HALVES, VH], F32, name=f"back{i}", tag=y_tag(i, 1))
+            for a in range(HALVES):
+                nc.tensor.transpose(back[:, a, :], turned_sb[:, a, :], ident[:])
+            z.append(back)
+        for i in range(PE_TILES, TILES):
+            pair = keep.tile([P, HALVES, 2, VH], F32, name=f"pair{i}")
+            zi = keep.tile([P, HALVES, VH], F32, name=f"z{i}")
+            nc.vector.tensor_tensor(out=pair[:], in0=ex[i][:, :, 0:2, :], in1=ex[i][:, :, 2:4, :], op=ALU.add)
+            nc.vector.tensor_tensor(out=zi[:], in0=pair[:, :, 0, :], in1=pair[:, :, 1, :], op=ALU.add)
+            z.append(zi)
+
+        for i in range(TILES):
+            res = keep.tile([P, HALVES, VH], F32, name=f"res{i}")
+            for a in range(HALVES):
+                nc.scalar.activation(out=res[:, a, :], in_=z[i][:, a, :], func=ACT.Ln, scale=weight[:, i, a : a + 1], bias=EPS)
+            nc.sync.dma_start(out=out[i * P : (i + 1) * P, :], in_=res[:].rearrange("p a v -> p (a v)"))

@@ -84,11 +84,11 @@ def tile_picked_ymatch_log_p_kernel(tc, x_words, x_scales, w1, e_words, e_scales
         nc.vector.tensor_copy(x_scale[:], xs_table[:].indirect(offs_sb[:]))
 
         w_bf = keep.tile([P, PACK * H], BF16, name="w_bf", align_bytes=64)
-        w_view = w_bf[:].rearrange("p (t m j) -> p m t j", t=PACK, j=PACK)
+        w_view = w_bf[:].rearrange("p (t m j) -> p m j t", t=PACK, j=PACK)
         for a, c in enumerate(w_cols):
             nc.scalar.activation(
                 out=w_view[:, c.start // PACK : c.stop // PACK],
-                in_=w_raw[a][:].rearrange("p j (m t) -> p m t j", t=PACK),
+                in_=w_raw[a][:].rearrange("p j (m t) -> p m j t", t=PACK),
                 func=ACT.Copy,
             )
         w_codes = keep.tile([P, H], U32, name="w_codes", align_bytes=64)

@@ -27,8 +27,9 @@ VH = V // HALVES
 LIST_ROWS = 16
 EPS = 1e-4
 MAX_GAP = 64.0
-W_SPLIT = 384
-E_ROW = 0
+W_SPLIT = 448
+E_ROW = 4
+E_FIRST = 768
 PE_TILES = 3
 
 
@@ -69,8 +70,8 @@ def tile_picked_ymatch_log_p_kernel(tc, x_words, x_scales, w1, e_words, e_scales
         make_identity(nc, ident[:])
 
         w_rows = w1.rearrange("(p j) c -> p j c", j=PACK)
-        nc.sync.dma_start(offs_sb[:], offs)
         load_words(nc, xw_table, x_words)
+        nc.sync.dma_start(offs_sb[:], offs)
         load_scale_rows(nc, xs_table, x_scales, 0)
         nc.sync.dma_start(sup_sb[:], sup)
         nc.sync.dma_start(out=w_raw[0][:], in_=w_rows[:, :, w_cols[0]])
@@ -93,14 +94,14 @@ def tile_picked_ymatch_log_p_kernel(tc, x_words, x_scales, w1, e_words, e_scales
             )
         w_codes = keep.tile([P, H], U32, name="w_codes", align_bytes=64)
         w_scale = keep.tile([P, H], U8, name="w_scale", align_bytes=64)
-        nc.vector.quantize_mx(out=w_codes[:].bitcast(FP8X4), scales=w_scale[:], in_=w_bf[:])
-
-        list_cols = HALF // LIST_ROWS
-        e_scale = []
         for a in range(HALVES):
-            es = keep.tile([P, HALF], U8, name=f"e_scale{a}", align_bytes=64)
-            nc.vector.tensor_copy(es[:], es_table[:].indirect(sup_sb[:, a * list_cols : (a + 1) * list_cols]))
-            e_scale.append(es)
+            cols = slice(a * H // HALVES, (a + 1) * H // HALVES)
+            nc.vector.quantize_mx(
+                out=w_codes[:, cols].bitcast(FP8X4), scales=w_scale[:, cols], in_=w_bf[:, PACK * cols.start : PACK * cols.stop]
+            )
+
+        e_scale = keep.tile([P, U], U8, name="e_scale", align_bytes=64)
+        nc.vector.tensor_copy(e_scale[:], es_table[:].indirect(sup_sb[:]))
 
         h_codes, h_scale = [], []
         for i in range(TILES):
@@ -127,16 +128,9 @@ def tile_picked_ymatch_log_p_kernel(tc, x_words, x_scales, w1, e_words, e_scales
             h_codes.append(hc)
             h_scale.append(hs)
 
-        e_codes = []
-        for a in range(HALVES):
-            ec = keep.tile([P, HALF], U32, name=f"e_codes{a}", align_bytes=64)
-            pieces = a + 1
-            for b in range(pieces):
-                lo = b * HALF // pieces
-                hi = (b + 1) * HALF // pieces
-                entries = sup_sb[:, (a * HALF + lo) // LIST_ROWS : (a * HALF + hi) // LIST_ROWS]
-                nc.vector.tensor_copy(ec[:, lo:hi], ew_table[:].indirect(entries))
-            e_codes.append(ec)
+        e_codes = keep.tile([P, U], U32, name="e_codes", align_bytes=64)
+        for lo, hi in ((0, E_FIRST), (E_FIRST, U)):
+            nc.vector.tensor_copy(e_codes[:, lo:hi], ew_table[:].indirect(sup_sb[:, lo // LIST_ROWS : hi // LIST_ROWS]))
 
         neg_max = keep.tile([P, TILES, HALVES], F32, name="neg_max")
         half_sum = keep.tile([P, TILES, HALVES], F32, name="half_sum")
@@ -148,8 +142,8 @@ def tile_picked_ymatch_log_p_kernel(tc, x_words, x_scales, w1, e_words, e_scales
                     out=bank[:],
                     lhsT=h_codes[i][:].bitcast(FP8X4),
                     lhsT_scale=h_scale[i][:],
-                    rhs=e_codes[a][:].bitcast(FP8X4),
-                    rhs_scale=e_scale[a][E_ROW:P, :],
+                    rhs=e_codes[:, a * HALF : (a + 1) * HALF].bitcast(FP8X4),
+                    rhs_scale=e_scale[E_ROW:P, a * HALF : (a + 1) * HALF],
                     start=True,
                     stop=True,
                 )
@@ -200,4 +194,7 @@ def tile_picked_ymatch_log_p_kernel(tc, x_words, x_scales, w1, e_words, e_scales
             res = keep.tile([P, HALVES, VH], F32, name=f"res{i}")
             for a in range(HALVES):
                 nc.scalar.activation(out=res[:, a, :], in_=z[i][:, a, :], func=ACT.Ln, scale=weight[:, i, a : a + 1], bias=EPS)
-            nc.sync.dma_start(out=out[i * P : (i + 1) * P, :], in_=res[:].rearrange("p a v -> p (a v)"))
+                if i == TILES - 1:
+                    nc.sync.dma_start(out=out[i * P : (i + 1) * P, a * VH : (a + 1) * VH], in_=res[:, a, :])
+            if i < TILES - 1:
+                nc.sync.dma_start(out=out[i * P : (i + 1) * P, :], in_=res[:].rearrange("p a v -> p (a v)"))

@@ -20,6 +20,8 @@ AX = mybir.AxisListType
 
 P = 128
 PACK = 4
+QUADRANTS = 4
+BANKS = 8
 TILES = S // P
 HALVES = 2
 HALF = U // HALVES
@@ -27,14 +29,14 @@ VH = V // HALVES
 LIST_ROWS = 16
 EPS = 1e-4
 MAX_GAP = 64.0
-W_SPLIT = 448
+W_SPLIT = 352
 E_ROW = 4
 E_FIRST = 768
-PE_TILES = 3
+PE_TILES = TILES - 1
 
 
 def load_scale_rows(nc, table, scales, row):
-    for q in range(4):
+    for q in range(QUADRANTS):
         nc.sync.dma_start(
             out=table[32 * q + row : 32 * q + row + 4, :].bitcast(I32),
             in_=scales[0, 4 * q : 4 * q + 4, :].bitcast(I32),
@@ -45,8 +47,8 @@ def load_words(nc, table, words):
     nc.sync.dma_start(out=table[:].bitcast(I32), in_=words[0].rearrange("p n t -> p (n t)").bitcast(I32))
 
 
-def y_tag(i, a):
-    return f"bank{(TILES + HALVES * i + a) % 8}"
+def logits_bank(i, a):
+    return f"bank{(TILES + HALVES * i + a) % BANKS}"
 
 
 def tile_picked_ymatch_log_p_kernel(tc, x_words, x_scales, w1, e_words, e_scales, offs, sup, out):
@@ -94,8 +96,7 @@ def tile_picked_ymatch_log_p_kernel(tc, x_words, x_scales, w1, e_words, e_scales
             )
         w_codes = keep.tile([P, H], U32, name="w_codes", align_bytes=64)
         w_scale = keep.tile([P, H], U8, name="w_scale", align_bytes=64)
-        for a in range(HALVES):
-            cols = slice(a * H // HALVES, (a + 1) * H // HALVES)
+        for cols in (slice(0, H // 2), slice(H // 2, H)):
             nc.vector.quantize_mx(
                 out=w_codes[:, cols].bitcast(FP8X4), scales=w_scale[:, cols], in_=w_bf[:, PACK * cols.start : PACK * cols.stop]
             )
@@ -137,7 +138,7 @@ def tile_picked_ymatch_log_p_kernel(tc, x_words, x_scales, w1, e_words, e_scales
         ex = [keep.tile([P, HALVES, D, VH], F32, name=f"ex{i}") for i in range(TILES)]
         for i in range(TILES):
             for a in range(HALVES):
-                bank = psum.tile([P, HALF], F32, name=f"y_bank{i}{a}", tag=y_tag(i, a))
+                bank = psum.tile([P, HALF], F32, name=f"y_bank{i}{a}", tag=logits_bank(i, a))
                 nc.tensor.matmul_mx(
                     out=bank[:],
                     lhsT=h_codes[i][:].bitcast(FP8X4),
@@ -171,7 +172,7 @@ def tile_picked_ymatch_log_p_kernel(tc, x_words, x_scales, w1, e_words, e_scales
 
         z = []
         for i in range(PE_TILES):
-            turned = psum.tile([P, HALVES, P], F32, name=f"turned{i}", tag=y_tag(i, 0))
+            turned = psum.tile([P, HALVES, P], F32, name=f"turned{i}", tag=logits_bank(i, 0))
             for a in range(HALVES):
                 for d in range(D):
                     nc.tensor.matmul(
@@ -179,22 +180,23 @@ def tile_picked_ymatch_log_p_kernel(tc, x_words, x_scales, w1, e_words, e_scales
                     )
             turned_sb = keep.tile([P, HALVES, P], F32, name=f"turned_sb{i}")
             nc.vector.tensor_copy(turned_sb[:], turned[:])
-            back = psum.tile([P, HALVES, VH], F32, name=f"back{i}", tag=y_tag(i, 1))
+            back = psum.tile([P, HALVES, VH], F32, name=f"back{i}", tag=logits_bank(i, 1))
             for a in range(HALVES):
                 nc.tensor.transpose(back[:, a, :], turned_sb[:, a, :], ident[:])
             z.append(back)
-        for i in range(PE_TILES, TILES):
-            pair = keep.tile([P, HALVES, 2, VH], F32, name=f"pair{i}")
-            zi = keep.tile([P, HALVES, VH], F32, name=f"z{i}")
-            nc.vector.tensor_tensor(out=pair[:], in0=ex[i][:, :, 0:2, :], in1=ex[i][:, :, 2:4, :], op=ALU.add)
-            nc.vector.tensor_tensor(out=zi[:], in0=pair[:, :, 0, :], in1=pair[:, :, 1, :], op=ALU.add)
-            z.append(zi)
+        last = TILES - 1
+        pair = keep.tile([P, HALVES, D // 2, VH], F32, name=f"pair{last}")
+        z_last = keep.tile([P, HALVES, VH], F32, name=f"z{last}")
+        nc.vector.tensor_tensor(out=pair[:], in0=ex[last][:, :, 0 : D // 2, :], in1=ex[last][:, :, D // 2 : D, :], op=ALU.add)
+        nc.vector.tensor_tensor(out=z_last[:], in0=pair[:, :, 0, :], in1=pair[:, :, 1, :], op=ALU.add)
+        z.append(z_last)
 
         for i in range(TILES):
+            rows = slice(i * P, (i + 1) * P)
             res = keep.tile([P, HALVES, VH], F32, name=f"res{i}")
             for a in range(HALVES):
                 nc.scalar.activation(out=res[:, a, :], in_=z[i][:, a, :], func=ACT.Ln, scale=weight[:, i, a : a + 1], bias=EPS)
-                if i == TILES - 1:
-                    nc.sync.dma_start(out=out[i * P : (i + 1) * P, a * VH : (a + 1) * VH], in_=res[:, a, :])
-            if i < TILES - 1:
-                nc.sync.dma_start(out=out[i * P : (i + 1) * P, :], in_=res[:].rearrange("p a v -> p (a v)"))
+                if i == last:
+                    nc.sync.dma_start(out=out[rows, a * VH : (a + 1) * VH], in_=res[:, a, :])
+            if i < last:
+                nc.sync.dma_start(out=out[rows, :], in_=res[:].rearrange("p a v -> p (a v)"))

@@ -67,23 +67,25 @@ def tile_picked_ymatch_log_p_kernel(tc, x_words, x_scales, w1, e_words, e_scales
         w_raw = [keep.tile([P, PACK, c.stop - c.start], F32, name=f"w_raw{a}") for a, c in enumerate(w_cols)]
 
         ident = keep.tile([P, P], F32, name="ident")
-        nc.vector.memset(xs_table[:].bitcast(I32), 0)
         nc.vector.memset(es_table[:].bitcast(I32), 0)
+        nc.vector.memset(xs_table[:].bitcast(I32), 0)
         make_identity(nc, ident[:])
 
         w_rows = w1.rearrange("(p j) c -> p j c", j=PACK)
         load_words(nc, xw_table, x_words)
         nc.sync.dma_start(offs_sb[:], offs)
-        load_scale_rows(nc, xs_table, x_scales, 0)
         nc.sync.dma_start(sup_sb[:], sup)
-        nc.sync.dma_start(out=w_raw[0][:], in_=w_rows[:, :, w_cols[0]])
         load_scale_rows(nc, es_table, e_scales, E_ROW)
+        nc.sync.dma_start(out=w_raw[0][:], in_=w_rows[:, :, w_cols[0]])
+        load_scale_rows(nc, xs_table, x_scales, 0)
         nc.sync.dma_start(out=w_raw[1][:], in_=w_rows[:, :, w_cols[1]])
         load_words(nc, ew_table, e_words)
 
         x_codes = keep.tile([P, S], U32, name="x_codes", align_bytes=64)
         x_scale = keep.tile([P, S], U8, name="x_scale", align_bytes=64)
         nc.vector.tensor_copy(x_codes[:], xw_table[:].indirect(offs_sb[:]))
+        e_scale = keep.tile([P, U], U8, name="e_scale", align_bytes=64)
+        nc.vector.tensor_copy(e_scale[:], es_table[:].indirect(sup_sb[:]))
         nc.vector.tensor_copy(x_scale[:], xs_table[:].indirect(offs_sb[:]))
 
         w_bf = keep.tile([P, PACK * H], BF16, name="w_bf", align_bytes=64)
@@ -100,9 +102,6 @@ def tile_picked_ymatch_log_p_kernel(tc, x_words, x_scales, w1, e_words, e_scales
             nc.vector.quantize_mx(
                 out=w_codes[:, cols].bitcast(FP8X4), scales=w_scale[:, cols], in_=w_bf[:, PACK * cols.start : PACK * cols.stop]
             )
-
-        e_scale = keep.tile([P, U], U8, name="e_scale", align_bytes=64)
-        nc.vector.tensor_copy(e_scale[:], es_table[:].indirect(sup_sb[:]))
 
         h_codes, h_scale = [], []
         for i in range(TILES):

@@ -43,8 +43,8 @@ def load_scale_rows(nc, table, scales, row):
         )
 
 
-def load_words(nc, table, words):
-    nc.sync.dma_start(out=table[:].bitcast(I32), in_=words[0].rearrange("p n t -> p (n t)").bitcast(I32))
+def load_words(queue, table, words):
+    queue.dma_start(out=table[:].bitcast(I32), in_=words[0].rearrange("p n t -> p (n t)").bitcast(I32))
 
 
 def logits_bank(i, a):
@@ -72,14 +72,14 @@ def tile_picked_ymatch_log_p_kernel(tc, x_words, x_scales, w1, e_words, e_scales
         make_identity(nc, ident[:])
 
         w_rows = w1.rearrange("(p j) c -> p j c", j=PACK)
-        load_words(nc, xw_table, x_words)
         nc.sync.dma_start(offs_sb[:], offs)
+        load_words(nc.scalar, xw_table, x_words)
         nc.sync.dma_start(sup_sb[:], sup)
         load_scale_rows(nc, es_table, e_scales, E_ROW)
         nc.sync.dma_start(out=w_raw[0][:], in_=w_rows[:, :, w_cols[0]])
         load_scale_rows(nc, xs_table, x_scales, 0)
         nc.sync.dma_start(out=w_raw[1][:], in_=w_rows[:, :, w_cols[1]])
-        load_words(nc, ew_table, e_words)
+        load_words(nc.sync, ew_table, e_words)
 
         x_codes = keep.tile([P, S], U32, name="x_codes", align_bytes=64)
         x_scale = keep.tile([P, S], U8, name="x_scale", align_bytes=64)

@@ -67,7 +67,8 @@ def tile_picked_ymatch_log_p_kernel(tc, x_words, x_scales, w1, e_words, e_scales
         w_raw = [keep.tile([P, PACK, c.stop - c.start], F32, name=f"w_raw{a}") for a, c in enumerate(w_cols)]
 
         ident = keep.tile([P, P], F32, name="ident")
-        nc.vector.memset(es_table[:].bitcast(I32), 0)
+        nc.vector.memset(es_table[:, 0 : W // 2].bitcast(I32), 0)
+        nc.gpsimd.memset(es_table[:, W // 2 : W].bitcast(I32), 0)
         nc.vector.memset(xs_table[:].bitcast(I32), 0)
         make_identity(nc, ident[:])
 
@@ -107,7 +108,7 @@ def tile_picked_ymatch_log_p_kernel(tc, x_words, x_scales, w1, e_words, e_scales
         for i in range(TILES):
             tok = slice(i * P, (i + 1) * P)
             bank = psum.tile([P, PACK * P], F32, name=f"h_bank{i}", tag=f"bank{i}")
-            for t in range(PACK):
+            for t in range(PACK) if i == 0 else reversed(range(PACK)):
                 nc.tensor.matmul_mx(
                     out=bank[:, t * P : (t + 1) * P],
                     lhsT=w_codes[:, t * P : (t + 1) * P].bitcast(FP8X4),

@@ -157,36 +157,43 @@ def tile_picked_ymatch_log_p_kernel(tc, x_words, x_scales, w1, e_words, e_scales
                     accum_out=half_sum[:, i, a : a + 1],
                 )
 
+        turned = []
+        for i in range(PE_TILES):
+            turned.append(psum.tile([P, HALVES, P], F32, name=f"turned{i}", tag=logits_bank(i, 0)))
+            for a in range(HALVES):
+                for d in range(D):
+                    nc.tensor.matmul(
+                        turned[i][:, a, :], lhsT=ex[i][:, a, d, :], rhs=ident[:], is_transpose=True, start=d == 0, stop=d == D - 1
+                    )
+
         gap = keep.tile([P, TILES, HALVES], F32, name="gap")
         clamped = keep.tile([P, TILES, HALVES], F32, name="clamped")
         factor = keep.tile([P, TILES, HALVES], F32, name="factor")
         other = keep.tile([P, TILES, HALVES], F32, name="other")
-        total = keep.tile([P, TILES, HALVES], F32, name="total")
         weight = keep.tile([P, TILES, HALVES], F32, name="weight")
         nc.vector.tensor_tensor(out=gap[:], in0=neg_max[:], in1=neg_max[:, :, ::-1], op=ALU.subtract)
         nc.vector.tensor_scalar_min(out=clamped[:], in0=gap[:], scalar1=MAX_GAP)
         nc.scalar.activation(out=factor[:], in_=clamped[:], func=ACT.Exp)
+
+        back_banks = [logits_bank(PE_TILES - 1, 1), logits_bank(PE_TILES, 0), logits_bank(0, 1)]
+
+        def turn_back(i):
+            turned_sb = keep.tile([P, HALVES, P], F32, name=f"turned_sb{i}")
+            nc.vector.tensor_copy(turned_sb[:], turned[i][:])
+            back = psum.tile([P, HALVES, VH], F32, name=f"back{i}", tag=back_banks[i])
+            for a in range(HALVES):
+                nc.tensor.transpose(back[:, a, :], turned_sb[:, a, :], ident[:])
+            return back
+
+        z = [turn_back(0)]
+        total = keep.tile([P, TILES, HALVES], F32, name="total", tag="turned_sb0")
         nc.vector.tensor_tensor(out=other[:], in0=factor[:], in1=half_sum[:, :, ::-1], op=ALU.mult)
         nc.vector.tensor_tensor(out=total[:], in0=other[:], in1=half_sum[:], op=ALU.add)
         nc.vector.reciprocal(out=weight[:], in_=total[:])
-
-        z = []
-        for i in range(PE_TILES):
-            turned = psum.tile([P, HALVES, P], F32, name=f"turned{i}", tag=logits_bank(i, 0))
-            for a in range(HALVES):
-                for d in range(D):
-                    nc.tensor.matmul(
-                        turned[:, a, :], lhsT=ex[i][:, a, d, :], rhs=ident[:], is_transpose=True, start=d == 0, stop=d == D - 1
-                    )
-            turned_sb = keep.tile([P, HALVES, P], F32, name=f"turned_sb{i}")
-            nc.vector.tensor_copy(turned_sb[:], turned[:])
-            back = psum.tile([P, HALVES, VH], F32, name=f"back{i}", tag=logits_bank(i, 1))
-            for a in range(HALVES):
-                nc.tensor.transpose(back[:, a, :], turned_sb[:, a, :], ident[:])
-            z.append(back)
+        z.extend(turn_back(i) for i in range(1, PE_TILES))
         last = TILES - 1
         pair = keep.tile([P, HALVES, D // 2, VH], F32, name=f"pair{last}")
-        z_last = keep.tile([P, HALVES, VH], F32, name=f"z{last}")
+        z_last = keep.tile([P, HALVES, VH], F32, name=f"z{last}", tag="turned_sb0")
         nc.vector.tensor_tensor(out=pair[:], in0=ex[last][:, :, 0 : D // 2, :], in1=ex[last][:, :, D // 2 : D, :], op=ALU.add)
         nc.vector.tensor_tensor(out=z_last[:], in0=pair[:, :, 0, :], in1=pair[:, :, 1, :], op=ALU.add)
         z.append(z_last)

@@ -29,9 +29,10 @@ VH = V // HALVES
 LIST_ROWS = 16
 EPS = 1e-4
 MAX_GAP = 64.0
-W_SPLIT = 352
+W_SPLIT = 272
 E_ROW = 4
-E_FIRST = 768
+E_ROWS = slice(16, 32)
+H_BUFS = 2
 PE_TILES = TILES - 1
 
 
@@ -55,6 +56,7 @@ def tile_picked_ymatch_log_p_kernel(tc, x_words, x_scales, w1, e_words, e_scales
     nc = tc.nc
     with ExitStack() as ctx:
         keep = ctx.enter_context(tc.tile_pool(name="keep", bufs=1))
+        reuse = ctx.enter_context(tc.tile_pool(name="reuse", bufs=1))
         psum = ctx.enter_context(tc.psum_pool(name="psum", bufs=1))
 
         offs_sb = keep.tile([P, S // LIST_ROWS], U16, name="offs_sb")
@@ -67,16 +69,19 @@ def tile_picked_ymatch_log_p_kernel(tc, x_words, x_scales, w1, e_words, e_scales
         w_raw = [keep.tile([P, PACK, c.stop - c.start], F32, name=f"w_raw{a}") for a, c in enumerate(w_cols)]
 
         ident = keep.tile([P, P], F32, name="ident")
-        nc.vector.memset(es_table[:, 0 : W // 2].bitcast(I32), 0)
-        nc.gpsimd.memset(es_table[:, W // 2 : W].bitcast(I32), 0)
         nc.vector.memset(xs_table[:].bitcast(I32), 0)
+        nc.gpsimd.memset(es_table[64:P, :].bitcast(I32), 0)
+        for lo, hi in ((0, E_ROWS.start), (E_ROWS.stop, 64)):
+            nc.vector.memset(es_table[lo:hi, :].bitcast(I32), 0)
+        e_scale = keep.tile([P, U], U8, name="e_scale", align_bytes=64)
+        nc.gpsimd.memset(e_scale[:].bitcast(I32), 0)
         make_identity(nc, ident[:])
 
         w_rows = w1.rearrange("(p j) c -> p j c", j=PACK)
-        nc.sync.dma_start(offs_sb[:], offs)
-        load_words(nc.scalar, xw_table, x_words)
         nc.sync.dma_start(sup_sb[:], sup)
-        load_scale_rows(nc, es_table, e_scales, E_ROW)
+        nc.scalar.dma_start(out=es_table[E_ROWS, :].bitcast(I32), in_=e_scales[0].bitcast(I32))
+        load_words(nc.sync, xw_table, x_words)
+        nc.sync.dma_start(offs_sb[:], offs)
         nc.sync.dma_start(out=w_raw[0][:], in_=w_rows[:, :, w_cols[0]])
         load_scale_rows(nc, xs_table, x_scales, 0)
         nc.sync.dma_start(out=w_raw[1][:], in_=w_rows[:, :, w_cols[1]])
@@ -84,9 +89,14 @@ def tile_picked_ymatch_log_p_kernel(tc, x_words, x_scales, w1, e_words, e_scales
 
         x_codes = keep.tile([P, S], U32, name="x_codes", align_bytes=64)
         x_scale = keep.tile([P, S], U8, name="x_scale", align_bytes=64)
+        e_rows = reuse.tile([P, U], U8, name="e_rows", align_bytes=64, offset=0)
+        nc.vector.tensor_copy(e_rows[:], es_table[:].indirect(sup_sb[:]))
+        for q in range(QUADRANTS):
+            nc.sync.dma_start(
+                out=e_scale[32 * q + E_ROW : 32 * q + E_ROW + 4, :].bitcast(I32),
+                in_=e_rows[E_ROWS.start + 4 * q : E_ROWS.start + 4 * q + 4, :].bitcast(I32),
+            )
         nc.vector.tensor_copy(x_codes[:], xw_table[:].indirect(offs_sb[:]))
-        e_scale = keep.tile([P, U], U8, name="e_scale", align_bytes=64)
-        nc.vector.tensor_copy(e_scale[:], es_table[:].indirect(sup_sb[:]))
         nc.vector.tensor_copy(x_scale[:], xs_table[:].indirect(offs_sb[:]))
 
         w_bf = keep.tile([P, PACK * H], BF16, name="w_bf", align_bytes=64)
@@ -104,7 +114,7 @@ def tile_picked_ymatch_log_p_kernel(tc, x_words, x_scales, w1, e_words, e_scales
                 out=w_codes[:, cols].bitcast(FP8X4), scales=w_scale[:, cols], in_=w_bf[:, PACK * cols.start : PACK * cols.stop]
             )
 
-        h_codes, h_scale = [], []
+        h_bf = []
         for i in range(TILES):
             tok = slice(i * P, (i + 1) * P)
             bank = psum.tile([P, PACK * P], F32, name=f"h_bank{i}", tag=f"bank{i}")
@@ -118,20 +128,31 @@ def tile_picked_ymatch_log_p_kernel(tc, x_words, x_scales, w1, e_words, e_scales
                     start=True,
                     stop=True,
                 )
-            h_bf = keep.tile([P, P * PACK], BF16, name=f"h_bf{i}", align_bytes=64)
+            h_bf.append(keep.tile([P, P * PACK], BF16, name=f"h_bf{i}", align_bytes=64))
             nc.scalar.copy(
-                out=h_bf[:].rearrange("p (n t) -> p n t", t=PACK),
+                out=h_bf[i][:].rearrange("p (n t) -> p n t", t=PACK),
                 in_=bank[:].rearrange("p (t n) -> p n t", t=PACK),
             )
-            hc = keep.tile([P, P], U32, name=f"h_codes{i}", align_bytes=64)
-            hs = keep.tile([P, P], U8, name=f"h_scale{i}", align_bytes=64)
-            nc.vector.quantize_mx(out=hc[:].bitcast(FP8X4), scales=hs[:], in_=h_bf[:])
-            h_codes.append(hc)
-            h_scale.append(hs)
 
-        e_codes = keep.tile([P, U], U32, name="e_codes", align_bytes=64)
-        for lo, hi in ((0, E_FIRST), (E_FIRST, U)):
-            nc.vector.tensor_copy(e_codes[:, lo:hi], ew_table[:].indirect(sup_sb[:, lo // LIST_ROWS : hi // LIST_ROWS]))
+        h_codes = []
+        h_scale = reuse.tile([P, TILES, P], U8, name="h_scale", align_bytes=64, offset=0)
+        e_codes = [
+            keep.tile([P, HALF], U32, name="e_codes0", align_bytes=64),
+            reuse.tile([P, HALF], U32, name="e_codes1", align_bytes=64, offset=S),
+        ]
+
+        def gather_e_words(a):
+            entries = slice(a * HALF // LIST_ROWS, (a + 1) * HALF // LIST_ROWS)
+            nc.vector.tensor_copy(e_codes[a][:], ew_table[:].indirect(sup_sb[:, entries]))
+
+        def quantize_h(i):
+            h_codes.append(keep.tile([P, P], U32, name=f"h_codes{i}", tag=f"h_codes{i % H_BUFS}", align_bytes=64))
+            nc.vector.quantize_mx(out=h_codes[i][:].bitcast(FP8X4), scales=h_scale[:, i, :], in_=h_bf[i][:])
+
+        gather_e_words(0)
+        quantize_h(0)
+        gather_e_words(1)
+        quantize_h(1)
 
         neg_max = keep.tile([P, TILES, HALVES], F32, name="neg_max")
         half_sum = keep.tile([P, TILES, HALVES], F32, name="half_sum")
@@ -142,8 +163,8 @@ def tile_picked_ymatch_log_p_kernel(tc, x_words, x_scales, w1, e_words, e_scales
                 nc.tensor.matmul_mx(
                     out=bank[:],
                     lhsT=h_codes[i][:].bitcast(FP8X4),
-                    lhsT_scale=h_scale[i][:],
-                    rhs=e_codes[:, a * HALF : (a + 1) * HALF].bitcast(FP8X4),
+                    lhsT_scale=h_scale[:, i, :],
+                    rhs=e_codes[a][:].bitcast(FP8X4),
                     rhs_scale=e_scale[E_ROW:P, a * HALF : (a + 1) * HALF],
                     start=True,
                     stop=True,
@@ -156,6 +177,8 @@ def tile_picked_ymatch_log_p_kernel(tc, x_words, x_scales, w1, e_words, e_scales
                     bias=neg_max[:, i, a : a + 1],
                     accum_out=half_sum[:, i, a : a + 1],
                 )
+            if i + H_BUFS < TILES:
+                quantize_h(i + H_BUFS)
 
         turned = []
         for i in range(PE_TILES):
@@ -166,14 +189,20 @@ def tile_picked_ymatch_log_p_kernel(tc, x_words, x_scales, w1, e_words, e_scales
                         turned[i][:, a, :], lhsT=ex[i][:, a, d, :], rhs=ident[:], is_transpose=True, start=d == 0, stop=d == D - 1
                     )
 
-        gap = keep.tile([P, TILES, HALVES], F32, name="gap")
-        clamped = keep.tile([P, TILES, HALVES], F32, name="clamped")
-        factor = keep.tile([P, TILES, HALVES], F32, name="factor")
-        other = keep.tile([P, TILES, HALVES], F32, name="other")
-        weight = keep.tile([P, TILES, HALVES], F32, name="weight")
-        nc.vector.tensor_tensor(out=gap[:], in0=neg_max[:], in1=neg_max[:, :, ::-1], op=ALU.subtract)
-        nc.vector.tensor_scalar_min(out=clamped[:], in0=gap[:], scalar1=MAX_GAP)
-        nc.scalar.activation(out=factor[:], in_=clamped[:], func=ACT.Exp)
+        gap = keep.tile([P, TILES], F32, name="gap")
+        factor = keep.tile([P, TILES], F32, name="factor")
+        other = keep.tile([P, TILES], F32, name="other")
+        weight = keep.tile([P, HALVES, TILES], F32, name="weight")
+        for i in range(TILES):
+            nc.vector.tensor_scalar(
+                out=gap[:, i : i + 1],
+                in0=neg_max[:, i, 0:1],
+                scalar1=neg_max[:, i, 1:2],
+                scalar2=MAX_GAP,
+                op0=ALU.subtract,
+                op1=ALU.min,
+            )
+        nc.scalar.activation(out=factor[:], in_=gap[:], func=ACT.Exp)
 
         back_banks = [logits_bank(PE_TILES - 1, 1), logits_bank(PE_TILES, 0), logits_bank(0, 1)]
 
@@ -185,25 +214,29 @@ def tile_picked_ymatch_log_p_kernel(tc, x_words, x_scales, w1, e_words, e_scales
                 nc.tensor.transpose(back[:, a, :], turned_sb[:, a, :], ident[:])
             return back
 
-        z = [turn_back(0)]
-        total = keep.tile([P, TILES, HALVES], F32, name="total", tag="turned_sb0")
-        nc.vector.tensor_tensor(out=other[:], in0=factor[:], in1=half_sum[:, :, ::-1], op=ALU.mult)
-        nc.vector.tensor_tensor(out=total[:], in0=other[:], in1=half_sum[:], op=ALU.add)
-        nc.vector.reciprocal(out=weight[:], in_=total[:])
-        z.extend(turn_back(i) for i in range(1, PE_TILES))
         last = TILES - 1
-        pair = keep.tile([P, HALVES, D // 2, VH], F32, name=f"pair{last}")
-        z_last = keep.tile([P, HALVES, VH], F32, name=f"z{last}", tag="turned_sb0")
-        nc.vector.tensor_tensor(out=pair[:], in0=ex[last][:, :, 0 : D // 2, :], in1=ex[last][:, :, D // 2 : D, :], op=ALU.add)
-        nc.vector.tensor_tensor(out=z_last[:], in0=pair[:, :, 0, :], in1=pair[:, :, 1, :], op=ALU.add)
-        z.append(z_last)
+        pair = keep.tile([P, HALVES, D // 2, VH], F32, name="pair")
+        z_last = keep.tile([P, HALVES, VH], F32, name="z_last")
 
-        for i in range(TILES):
+        def add_last(a):
+            nc.vector.tensor_tensor(out=pair[:, a], in0=ex[last][:, a, 0 : D // 2, :], in1=ex[last][:, a, D // 2 : D, :], op=ALU.add)
+            nc.vector.tensor_tensor(out=z_last[:, a, :], in0=pair[:, a, 0, :], in1=pair[:, a, 1, :], op=ALU.add)
+
+        add_last(0)
+        total = keep.tile([P, TILES], F32, name="total")
+        nc.vector.tensor_tensor(out=other[:], in0=factor[:], in1=half_sum[:, :, 1], op=ALU.mult)
+        nc.vector.tensor_tensor(out=total[:], in0=other[:], in1=half_sum[:, :, 0], op=ALU.add)
+        nc.vector.reciprocal(out=weight[:, 0, :], in_=total[:])
+        nc.vector.tensor_tensor(out=weight[:, 1, :], in0=factor[:], in1=weight[:, 0, :], op=ALU.mult)
+        z = [turn_back(i) for i in range(PE_TILES)] + [z_last]
+        add_last(1)
+
+        res = [keep.tile([P, HALVES, VH], F32, name=f"res{i}") for i in range(TILES)]
+        order = [(last, 0)] + [(i, a) for i in range(last - 1) for a in range(HALVES)] + [(last, 1), (last - 1, 0), (last - 1, 1)]
+        for i, a in order:
             rows = slice(i * P, (i + 1) * P)
-            res = keep.tile([P, HALVES, VH], F32, name=f"res{i}")
-            for a in range(HALVES):
-                nc.scalar.activation(out=res[:, a, :], in_=z[i][:, a, :], func=ACT.Ln, scale=weight[:, i, a : a + 1], bias=EPS)
-                if i == last:
-                    nc.sync.dma_start(out=out[rows, a * VH : (a + 1) * VH], in_=res[:, a, :])
-            if i < last:
-                nc.sync.dma_start(out=out[rows, :], in_=res[:].rearrange("p a v -> p (a v)"))
+            nc.scalar.activation(out=res[i][:, a, :], in_=z[i][:, a, :], func=ACT.Ln, scale=weight[:, a, i : i + 1], bias=EPS)
+            if i >= last - 1:
+                nc.sync.dma_start(out=out[rows, a * VH : (a + 1) * VH], in_=res[i][:, a, :])
+            elif a == HALVES - 1:
+                nc.sync.dma_start(out=out[rows, :], in_=res[i][:].rearrange("p a v -> p (a v)"))

@@ -31,9 +31,8 @@ EPS = 1e-4
 MAX_GAP = 64.0
 W_SPLIT = 272
 E_ROW = 4
-E_ROWS = slice(16, 32)
+E_ROWS = slice(P - 16, P)
 H_BUFS = 2
-PE_TILES = TILES - 1
 
 
 def load_scale_rows(nc, table, scales, row):
@@ -70,11 +69,9 @@ def tile_picked_ymatch_log_p_kernel(tc, x_words, x_scales, w1, e_words, e_scales
 
         ident = keep.tile([P, P], F32, name="ident")
         nc.vector.memset(xs_table[:].bitcast(I32), 0)
-        nc.gpsimd.memset(es_table[64:P, :].bitcast(I32), 0)
-        for lo, hi in ((0, E_ROWS.start), (E_ROWS.stop, 64)):
-            nc.vector.memset(es_table[lo:hi, :].bitcast(I32), 0)
+        nc.vector.memset(es_table[0 : E_ROWS.start, :].bitcast(I32), 0)
         e_scale = keep.tile([P, U], U8, name="e_scale", align_bytes=64)
-        nc.gpsimd.memset(e_scale[:].bitcast(I32), 0)
+        nc.vector.memset(e_scale[:].bitcast(I32), 0)
         make_identity(nc, ident[:])
 
         w_rows = w1.rearrange("(p j) c -> p j c", j=PACK)
@@ -180,14 +177,23 @@ def tile_picked_ymatch_log_p_kernel(tc, x_words, x_scales, w1, e_words, e_scales
             if i + H_BUFS < TILES:
                 quantize_h(i + H_BUFS)
 
-        turned = []
-        for i in range(PE_TILES):
-            turned.append(psum.tile([P, HALVES, P], F32, name=f"turned{i}", tag=logits_bank(i, 0)))
-            for a in range(HALVES):
-                for d in range(D):
-                    nc.tensor.matmul(
-                        turned[i][:, a, :], lhsT=ex[i][:, a, d, :], rhs=ident[:], is_transpose=True, start=d == 0, stop=d == D - 1
-                    )
+        groups = [(0, 1), (2,)]
+        turned = [
+            psum.tile([P, 2, HALVES, P], F32, name="turned01", tag=logits_bank(1, 1)),
+            psum.tile([P, 1, HALVES, P], F32, name="turned2", tag=logits_bank(2, 0)),
+        ]
+        for g, group in enumerate(groups):
+            for n, i in enumerate(group):
+                for a in range(HALVES):
+                    for d in range(D):
+                        nc.tensor.matmul(
+                            turned[g][:, n, a, :],
+                            lhsT=ex[i][:, a, d, :],
+                            rhs=ident[:],
+                            is_transpose=True,
+                            start=d == 0,
+                            stop=d == D - 1,
+                        )
 
         gap = keep.tile([P, TILES], F32, name="gap")
         factor = keep.tile([P, TILES], F32, name="factor")
@@ -204,15 +210,17 @@ def tile_picked_ymatch_log_p_kernel(tc, x_words, x_scales, w1, e_words, e_scales
             )
         nc.scalar.activation(out=factor[:], in_=gap[:], func=ACT.Exp)
 
-        back_banks = [logits_bank(PE_TILES - 1, 1), logits_bank(PE_TILES, 0), logits_bank(0, 1)]
+        back_banks = [logits_bank(0, 0), logits_bank(0, 1), logits_bank(1, 0)]
 
-        def turn_back(i):
-            turned_sb = keep.tile([P, HALVES, P], F32, name=f"turned_sb{i}")
-            nc.vector.tensor_copy(turned_sb[:], turned[i][:])
-            back = psum.tile([P, HALVES, VH], F32, name=f"back{i}", tag=back_banks[i])
-            for a in range(HALVES):
-                nc.tensor.transpose(back[:, a, :], turned_sb[:, a, :], ident[:])
-            return back
+        def turn_back(g):
+            turned_sb = keep.tile([P, len(groups[g]), HALVES, P], F32, name=f"turned_sb{g}")
+            nc.vector.tensor_copy(turned_sb[:], turned[g][:])
+            backs = []
+            for n, i in enumerate(groups[g]):
+                backs.append(psum.tile([P, HALVES, VH], F32, name=f"back{i}", tag=back_banks[i]))
+                for a in range(HALVES):
+                    nc.tensor.transpose(backs[n][:, a, :], turned_sb[:, n, a, :], ident[:])
+            return backs
 
         last = TILES - 1
         pair = keep.tile([P, HALVES, D // 2, VH], F32, name="pair")
@@ -228,7 +236,7 @@ def tile_picked_ymatch_log_p_kernel(tc, x_words, x_scales, w1, e_words, e_scales
         nc.vector.tensor_tensor(out=total[:], in0=other[:], in1=half_sum[:, :, 0], op=ALU.add)
         nc.vector.reciprocal(out=weight[:, 0, :], in_=total[:])
         nc.vector.tensor_tensor(out=weight[:, 1, :], in0=factor[:], in1=weight[:, 0, :], op=ALU.mult)
-        z = [turn_back(i) for i in range(PE_TILES)] + [z_last]
+        z = turn_back(0) + turn_back(1) + [z_last]
         add_last(1)
 
         res = [keep.tile([P, HALVES, VH], F32, name=f"res{i}") for i in range(TILES)]

@@ -29,7 +29,7 @@ VH = V // HALVES
 LIST_ROWS = 16
 EPS = 1e-4
 MAX_GAP = 64.0
-W_SPLIT = 272
+W_SPLIT = 256
 E_ROW = 4
 E_ROWS = slice(P - 16, P)
 H_BUFS = 2
@@ -138,44 +138,54 @@ def tile_picked_ymatch_log_p_kernel(tc, x_words, x_scales, w1, e_words, e_scales
             reuse.tile([P, HALF], U32, name="e_codes1", align_bytes=64, offset=S),
         ]
 
-        def gather_e_words(a):
-            entries = slice(a * HALF // LIST_ROWS, (a + 1) * HALF // LIST_ROWS)
-            nc.vector.tensor_copy(e_codes[a][:], ew_table[:].indirect(sup_sb[:, entries]))
+        def gather_e_words(a, lo, hi):
+            entries = slice((a * HALF + lo) // LIST_ROWS, (a * HALF + hi) // LIST_ROWS)
+            nc.vector.tensor_copy(e_codes[a][:, lo:hi], ew_table[:].indirect(sup_sb[:, entries]))
 
         def quantize_h(i):
             h_codes.append(keep.tile([P, P], U32, name=f"h_codes{i}", tag=f"h_codes{i % H_BUFS}", align_bytes=64))
             nc.vector.quantize_mx(out=h_codes[i][:].bitcast(FP8X4), scales=h_scale[:, i, :], in_=h_bf[i][:])
 
-        gather_e_words(0)
+        gather_e_words(0, 0, HALF)
         quantize_h(0)
-        gather_e_words(1)
+        gather_e_words(1, 0, HALF // 2)
         quantize_h(1)
+        gather_e_words(1, HALF // 2, HALF)
 
         neg_max = keep.tile([P, TILES, HALVES], F32, name="neg_max")
         half_sum = keep.tile([P, TILES, HALVES], F32, name="half_sum")
         ex = [keep.tile([P, HALVES, D, VH], F32, name=f"ex{i}") for i in range(TILES)]
-        for i in range(TILES):
-            for a in range(HALVES):
-                bank = psum.tile([P, HALF], F32, name=f"y_bank{i}{a}", tag=logits_bank(i, a))
-                nc.tensor.matmul_mx(
-                    out=bank[:],
-                    lhsT=h_codes[i][:].bitcast(FP8X4),
-                    lhsT_scale=h_scale[:, i, :],
-                    rhs=e_codes[a][:].bitcast(FP8X4),
-                    rhs_scale=e_scale[E_ROW:P, a * HALF : (a + 1) * HALF],
-                    start=True,
-                    stop=True,
-                )
-                nc.vector.tensor_reduce(out=neg_max[:, i, a : a + 1], in_=bank[:], axis=AX.X, op=ALU.max, negate=True)
-                nc.scalar.activation(
-                    out=ex[i][:, a],
-                    in_=bank[:].rearrange("p (v d) -> p d v", d=D),
-                    func=ACT.Exp,
-                    bias=neg_max[:, i, a : a + 1],
-                    accum_out=half_sum[:, i, a : a + 1],
-                )
-            if i + H_BUFS < TILES:
-                quantize_h(i + H_BUFS)
+        steps = [(i, a) for a in range(HALVES) for i in range(H_BUFS)] + [(i, a) for i in range(H_BUFS, TILES) for a in range(HALVES)]
+        quantize_after = {(1, 0): 2, (1, 1): 3}
+        banks = {}
+
+        def logits(i, a):
+            banks[i, a] = psum.tile([P, HALF], F32, name=f"y_bank{i}{a}", tag=logits_bank(i, a))
+            nc.tensor.matmul_mx(
+                out=banks[i, a][:],
+                lhsT=h_codes[i][:].bitcast(FP8X4),
+                lhsT_scale=h_scale[:, i, :],
+                rhs=e_codes[a][:].bitcast(FP8X4),
+                rhs_scale=e_scale[E_ROW:P, a * HALF : (a + 1) * HALF],
+                start=True,
+                stop=True,
+            )
+
+        for i, a in steps[: H_BUFS * HALVES]:
+            logits(i, a)
+        for i, a in steps:
+            nc.vector.tensor_reduce(out=neg_max[:, i, a : a + 1], in_=banks[i, a][:], axis=AX.X, op=ALU.max, negate=True)
+            nc.scalar.activation(
+                out=ex[i][:, a],
+                in_=banks[i, a][:].rearrange("p (v d) -> p d v", d=D),
+                func=ACT.Exp,
+                bias=neg_max[:, i, a : a + 1],
+                accum_out=half_sum[:, i, a : a + 1],
+            )
+            if (i, a) in quantize_after:
+                quantize_h(quantize_after[i, a])
+                for b in range(HALVES):
+                    logits(quantize_after[i, a], b)
 
         groups = [(0, 1), (2,)]
         turned = [

@@ -29,7 +29,7 @@ VH = V // HALVES
 LIST_ROWS = 16
 EPS = 1e-4
 MAX_GAP = 64.0
-W_SPLIT = 256
+W_SPLIT = 304
 E_ROW = 4
 E_ROWS = slice(P - 16, P)
 H_BUFS = 2
@@ -77,9 +77,9 @@ def tile_picked_ymatch_log_p_kernel(tc, x_words, x_scales, w1, e_words, e_scales
         w_rows = w1.rearrange("(p j) c -> p j c", j=PACK)
         nc.sync.dma_start(sup_sb[:], sup)
         nc.scalar.dma_start(out=es_table[E_ROWS, :].bitcast(I32), in_=e_scales[0].bitcast(I32))
+        nc.sync.dma_start(out=w_raw[0][:], in_=w_rows[:, :, w_cols[0]])
         load_words(nc.sync, xw_table, x_words)
         nc.sync.dma_start(offs_sb[:], offs)
-        nc.sync.dma_start(out=w_raw[0][:], in_=w_rows[:, :, w_cols[0]])
         load_scale_rows(nc, xs_table, x_scales, 0)
         nc.sync.dma_start(out=w_raw[1][:], in_=w_rows[:, :, w_cols[1]])
         load_words(nc.sync, ew_table, e_words)

@@ -32,7 +32,7 @@ MAX_GAP = 64.0
 W_SPLIT = 304
 E_ROW = 4
 E_ROWS = slice(P - 16, P)
-H_BUFS = 2
+PE_TILES = TILES - 1
 
 
 def load_scale_rows(nc, table, scales, row):
@@ -138,123 +138,91 @@ def tile_picked_ymatch_log_p_kernel(tc, x_words, x_scales, w1, e_words, e_scales
             reuse.tile([P, HALF], U32, name="e_codes1", align_bytes=64, offset=S),
         ]
 
-        def gather_e_words(a, lo, hi):
-            entries = slice((a * HALF + lo) // LIST_ROWS, (a * HALF + hi) // LIST_ROWS)
-            nc.vector.tensor_copy(e_codes[a][:, lo:hi], ew_table[:].indirect(sup_sb[:, entries]))
+        def gather_e_words(a):
+            entries = slice(a * HALF // LIST_ROWS, (a + 1) * HALF // LIST_ROWS)
+            nc.vector.tensor_copy(e_codes[a][:], ew_table[:].indirect(sup_sb[:, entries]))
 
         def quantize_h(i):
-            h_codes.append(keep.tile([P, P], U32, name=f"h_codes{i}", tag=f"h_codes{i % H_BUFS}", align_bytes=64))
+            h_codes.append(keep.tile([P, P], U32, name=f"h_codes{i}", align_bytes=64))
             nc.vector.quantize_mx(out=h_codes[i][:].bitcast(FP8X4), scales=h_scale[:, i, :], in_=h_bf[i][:])
 
-        gather_e_words(0, 0, HALF)
+        gather_e_words(0)
         quantize_h(0)
-        gather_e_words(1, 0, HALF // 2)
-        quantize_h(1)
-        gather_e_words(1, HALF // 2, HALF)
+        gather_e_words(1)
+        for i in range(1, TILES):
+            quantize_h(i)
 
         neg_max = keep.tile([P, TILES, HALVES], F32, name="neg_max")
         half_sum = keep.tile([P, TILES, HALVES], F32, name="half_sum")
         ex = [keep.tile([P, HALVES, D, VH], F32, name=f"ex{i}") for i in range(TILES)]
-        steps = [(i, a) for a in range(HALVES) for i in range(H_BUFS)] + [(i, a) for i in range(H_BUFS, TILES) for a in range(HALVES)]
-        quantize_after = {(1, 0): 2, (1, 1): 3}
-        banks = {}
-
-        def logits(i, a):
-            banks[i, a] = psum.tile([P, HALF], F32, name=f"y_bank{i}{a}", tag=logits_bank(i, a))
-            nc.tensor.matmul_mx(
-                out=banks[i, a][:],
-                lhsT=h_codes[i][:].bitcast(FP8X4),
-                lhsT_scale=h_scale[:, i, :],
-                rhs=e_codes[a][:].bitcast(FP8X4),
-                rhs_scale=e_scale[E_ROW:P, a * HALF : (a + 1) * HALF],
-                start=True,
-                stop=True,
-            )
-
-        for i, a in steps[: H_BUFS * HALVES]:
-            logits(i, a)
-        for i, a in steps:
-            nc.vector.tensor_reduce(out=neg_max[:, i, a : a + 1], in_=banks[i, a][:], axis=AX.X, op=ALU.max, negate=True)
-            nc.scalar.activation(
-                out=ex[i][:, a],
-                in_=banks[i, a][:].rearrange("p (v d) -> p d v", d=D),
-                func=ACT.Exp,
-                bias=neg_max[:, i, a : a + 1],
-                accum_out=half_sum[:, i, a : a + 1],
-            )
-            if (i, a) in quantize_after:
-                quantize_h(quantize_after[i, a])
-                for b in range(HALVES):
-                    logits(quantize_after[i, a], b)
-
-        groups = [(0, 1), (2,)]
-        turned = [
-            psum.tile([P, 2, HALVES, P], F32, name="turned01", tag=logits_bank(1, 1)),
-            psum.tile([P, 1, HALVES, P], F32, name="turned2", tag=logits_bank(2, 0)),
-        ]
-        for g, group in enumerate(groups):
-            for n, i in enumerate(group):
-                for a in range(HALVES):
-                    for d in range(D):
-                        nc.tensor.matmul(
-                            turned[g][:, n, a, :],
-                            lhsT=ex[i][:, a, d, :],
-                            rhs=ident[:],
-                            is_transpose=True,
-                            start=d == 0,
-                            stop=d == D - 1,
-                        )
-
-        gap = keep.tile([P, TILES], F32, name="gap")
-        factor = keep.tile([P, TILES], F32, name="factor")
-        other = keep.tile([P, TILES], F32, name="other")
-        weight = keep.tile([P, HALVES, TILES], F32, name="weight")
         for i in range(TILES):
-            nc.vector.tensor_scalar(
-                out=gap[:, i : i + 1],
-                in0=neg_max[:, i, 0:1],
-                scalar1=neg_max[:, i, 1:2],
-                scalar2=MAX_GAP,
-                op0=ALU.subtract,
-                op1=ALU.min,
-            )
-        nc.scalar.activation(out=factor[:], in_=gap[:], func=ACT.Exp)
+            for a in range(HALVES):
+                bank = psum.tile([P, HALF], F32, name=f"y_bank{i}{a}", tag=logits_bank(i, a))
+                nc.tensor.matmul_mx(
+                    out=bank[:],
+                    lhsT=h_codes[i][:].bitcast(FP8X4),
+                    lhsT_scale=h_scale[:, i, :],
+                    rhs=e_codes[a][:].bitcast(FP8X4),
+                    rhs_scale=e_scale[E_ROW:P, a * HALF : (a + 1) * HALF],
+                    start=True,
+                    stop=True,
+                )
+                nc.vector.tensor_reduce(out=neg_max[:, i, a : a + 1], in_=bank[:], axis=AX.X, op=ALU.max, negate=True)
+                nc.scalar.activation(
+                    out=ex[i][:, a],
+                    in_=bank[:].rearrange("p (v d) -> p d v", d=D),
+                    func=ACT.Exp,
+                    bias=neg_max[:, i, a : a + 1],
+                    accum_out=half_sum[:, i, a : a + 1],
+                )
 
-        back_banks = [logits_bank(0, 0), logits_bank(0, 1), logits_bank(1, 0)]
+        turned = []
+        for i in range(PE_TILES):
+            turned.append(psum.tile([P, HALVES, P], F32, name=f"turned{i}", tag=logits_bank(i, 0)))
+            for a in range(HALVES):
+                for d in range(D):
+                    nc.tensor.matmul(
+                        turned[i][:, a, :], lhsT=ex[i][:, a, d, :], rhs=ident[:], is_transpose=True, start=d == 0, stop=d == D - 1
+                    )
 
-        def turn_back(g):
-            turned_sb = keep.tile([P, len(groups[g]), HALVES, P], F32, name=f"turned_sb{g}")
-            nc.vector.tensor_copy(turned_sb[:], turned[g][:])
-            backs = []
-            for n, i in enumerate(groups[g]):
-                backs.append(psum.tile([P, HALVES, VH], F32, name=f"back{i}", tag=back_banks[i]))
-                for a in range(HALVES):
-                    nc.tensor.transpose(backs[n][:, a, :], turned_sb[:, n, a, :], ident[:])
-            return backs
+        gap = keep.tile([P, TILES, HALVES], F32, name="gap")
+        clamped = keep.tile([P, TILES, HALVES], F32, name="clamped")
+        factor = keep.tile([P, TILES, HALVES], F32, name="factor")
+        other = keep.tile([P, TILES, HALVES], F32, name="other")
+        weight = keep.tile([P, TILES, HALVES], F32, name="weight")
+        nc.vector.tensor_tensor(out=gap[:], in0=neg_max[:], in1=neg_max[:, :, ::-1], op=ALU.subtract)
+        nc.vector.tensor_scalar_min(out=clamped[:], in0=gap[:], scalar1=MAX_GAP)
+        nc.scalar.activation(out=factor[:], in_=clamped[:], func=ACT.Exp)
 
+        back_banks = [logits_bank(PE_TILES - 1, 1), logits_bank(PE_TILES, 0), logits_bank(0, 1)]
+
+        def turn_back(i):
+            turned_sb = keep.tile([P, HALVES, P], F32, name=f"turned_sb{i}")
+            nc.vector.tensor_copy(turned_sb[:], turned[i][:])
+            back = psum.tile([P, HALVES, VH], F32, name=f"back{i}", tag=back_banks[i])
+            for a in range(HALVES):
+                nc.tensor.transpose(back[:, a, :], turned_sb[:, a, :], ident[:])
+            return back
+
+        z = [turn_back(0)]
+        total = keep.tile([P, TILES, HALVES], F32, name="total", tag="turned_sb0")
+        nc.vector.tensor_tensor(out=other[:], in0=factor[:], in1=half_sum[:, :, ::-1], op=ALU.mult)
+        nc.vector.tensor_tensor(out=total[:], in0=other[:], in1=half_sum[:], op=ALU.add)
+        nc.vector.reciprocal(out=weight[:], in_=total[:])
+        z.extend(turn_back(i) for i in range(1, PE_TILES))
         last = TILES - 1
-        pair = keep.tile([P, HALVES, D // 2, VH], F32, name="pair")
-        z_last = keep.tile([P, HALVES, VH], F32, name="z_last")
+        pair = keep.tile([P, HALVES, D // 2, VH], F32, name=f"pair{last}")
+        z_last = keep.tile([P, HALVES, VH], F32, name=f"z{last}", tag="turned_sb0")
+        nc.vector.tensor_tensor(out=pair[:], in0=ex[last][:, :, 0 : D // 2, :], in1=ex[last][:, :, D // 2 : D, :], op=ALU.add)
+        nc.vector.tensor_tensor(out=z_last[:], in0=pair[:, :, 0, :], in1=pair[:, :, 1, :], op=ALU.add)
+        z.append(z_last)
 
-        def add_last(a):
-            nc.vector.tensor_tensor(out=pair[:, a], in0=ex[last][:, a, 0 : D // 2, :], in1=ex[last][:, a, D // 2 : D, :], op=ALU.add)
-            nc.vector.tensor_tensor(out=z_last[:, a, :], in0=pair[:, a, 0, :], in1=pair[:, a, 1, :], op=ALU.add)
-
-        add_last(0)
-        total = keep.tile([P, TILES], F32, name="total")
-        nc.vector.tensor_tensor(out=other[:], in0=factor[:], in1=half_sum[:, :, 1], op=ALU.mult)
-        nc.vector.tensor_tensor(out=total[:], in0=other[:], in1=half_sum[:, :, 0], op=ALU.add)
-        nc.vector.reciprocal(out=weight[:, 0, :], in_=total[:])
-        nc.vector.tensor_tensor(out=weight[:, 1, :], in0=factor[:], in1=weight[:, 0, :], op=ALU.mult)
-        z = turn_back(0) + turn_back(1) + [z_last]
-        add_last(1)
-
-        res = [keep.tile([P, HALVES, VH], F32, name=f"res{i}") for i in range(TILES)]
-        order = [(last, 0)] + [(i, a) for i in range(last - 1) for a in range(HALVES)] + [(last, 1), (last - 1, 0), (last - 1, 1)]
-        for i, a in order:
+        for i in range(TILES):
             rows = slice(i * P, (i + 1) * P)
-            nc.scalar.activation(out=res[i][:, a, :], in_=z[i][:, a, :], func=ACT.Ln, scale=weight[:, a, i : i + 1], bias=EPS)
-            if i >= last - 1:
-                nc.sync.dma_start(out=out[rows, a * VH : (a + 1) * VH], in_=res[i][:, a, :])
-            elif a == HALVES - 1:
-                nc.sync.dma_start(out=out[rows, :], in_=res[i][:].rearrange("p a v -> p (a v)"))
+            res = keep.tile([P, HALVES, VH], F32, name=f"res{i}")
+            for a in range(HALVES):
+                nc.scalar.activation(out=res[:, a, :], in_=z[i][:, a, :], func=ACT.Ln, scale=weight[:, i, a : a + 1], bias=EPS)
+                if i == last:
+                    nc.sync.dma_start(out=out[rows, a * VH : (a + 1) * VH], in_=res[:, a, :])
+            if i < last:
+                nc.sync.dma_start(out=out[rows, :], in_=res[:].rearrange("p a v -> p (a v)"))

@@ -29,7 +29,7 @@ VH = V // HALVES
 LIST_ROWS = 16
 EPS = 1e-4
 MAX_GAP = 64.0
-W_SPLIT = 304
+W_SPLIT = 272
 E_ROW = 4
 E_ROWS = slice(P - 16, P)
 PE_TILES = TILES - 1
@@ -143,13 +143,13 @@ def tile_picked_ymatch_log_p_kernel(tc, x_words, x_scales, w1, e_words, e_scales
             nc.vector.tensor_copy(e_codes[a][:], ew_table[:].indirect(sup_sb[:, entries]))
 
         def quantize_h(i):
-            h_codes.append(keep.tile([P, P], U32, name=f"h_codes{i}", align_bytes=64))
+            h_codes.append(keep.tile([P, P], U32, name=f"h_codes{i}", tag=f"h_codes{i % (TILES - 1)}", align_bytes=64))
             nc.vector.quantize_mx(out=h_codes[i][:].bitcast(FP8X4), scales=h_scale[:, i, :], in_=h_bf[i][:])
 
         gather_e_words(0)
         quantize_h(0)
         gather_e_words(1)
-        for i in range(1, TILES):
+        for i in range(1, TILES - 1):
             quantize_h(i)
 
         neg_max = keep.tile([P, TILES, HALVES], F32, name="neg_max")
@@ -175,6 +175,8 @@ def tile_picked_ymatch_log_p_kernel(tc, x_words, x_scales, w1, e_words, e_scales
                     bias=neg_max[:, i, a : a + 1],
                     accum_out=half_sum[:, i, a : a + 1],
                 )
+            if i == 0:
+                quantize_h(TILES - 1)
 
         turned = []
         for i in range(PE_TILES):

@@ -32,6 +32,7 @@ MAX_GAP = 64.0
 W_SPLIT = 272
 E_ROW = 4
 E_ROWS = slice(P - 16, P)
+E_FIRST = 768
 PE_TILES = TILES - 1
 
 
@@ -133,22 +134,20 @@ def tile_picked_ymatch_log_p_kernel(tc, x_words, x_scales, w1, e_words, e_scales
 
         h_codes = []
         h_scale = reuse.tile([P, TILES, P], U8, name="h_scale", align_bytes=64, offset=0)
-        e_codes = [
-            keep.tile([P, HALF], U32, name="e_codes0", align_bytes=64),
-            reuse.tile([P, HALF], U32, name="e_codes1", align_bytes=64, offset=S),
+        e_first = keep.tile([P, E_FIRST], U32, name="e_first", align_bytes=64)
+        e_rest = reuse.tile([P, U - E_FIRST], U32, name="e_rest", align_bytes=64, offset=S)
+        passes = [
+            [(e_first[:, 0:HALF], 0, HALF)],
+            [(e_first[:, HALF:E_FIRST], HALF, E_FIRST - HALF), (e_rest[:], E_FIRST, U - E_FIRST)],
         ]
-
-        def gather_e_words(a):
-            entries = slice(a * HALF // LIST_ROWS, (a + 1) * HALF // LIST_ROWS)
-            nc.vector.tensor_copy(e_codes[a][:], ew_table[:].indirect(sup_sb[:, entries]))
 
         def quantize_h(i):
             h_codes.append(keep.tile([P, P], U32, name=f"h_codes{i}", tag=f"h_codes{i % (TILES - 1)}", align_bytes=64))
             nc.vector.quantize_mx(out=h_codes[i][:].bitcast(FP8X4), scales=h_scale[:, i, :], in_=h_bf[i][:])
 
-        gather_e_words(0)
+        nc.vector.tensor_copy(e_first[:], ew_table[:].indirect(sup_sb[:, 0 : E_FIRST // LIST_ROWS]))
         quantize_h(0)
-        gather_e_words(1)
+        nc.vector.tensor_copy(e_rest[:], ew_table[:].indirect(sup_sb[:, E_FIRST // LIST_ROWS : U // LIST_ROWS]))
         for i in range(1, TILES - 1):
             quantize_h(i)
 
@@ -158,15 +157,16 @@ def tile_picked_ymatch_log_p_kernel(tc, x_words, x_scales, w1, e_words, e_scales
         for i in range(TILES):
             for a in range(HALVES):
                 bank = psum.tile([P, HALF], F32, name=f"y_bank{i}{a}", tag=logits_bank(i, a))
-                nc.tensor.matmul_mx(
-                    out=bank[:],
-                    lhsT=h_codes[i][:].bitcast(FP8X4),
-                    lhsT_scale=h_scale[:, i, :],
-                    rhs=e_codes[a][:].bitcast(FP8X4),
-                    rhs_scale=e_scale[E_ROW:P, a * HALF : (a + 1) * HALF],
-                    start=True,
-                    stop=True,
-                )
+                for codes, first, count in passes[a]:
+                    nc.tensor.matmul_mx(
+                        out=bank[:, first - a * HALF : first - a * HALF + count],
+                        lhsT=h_codes[i][:].bitcast(FP8X4),
+                        lhsT_scale=h_scale[:, i, :],
+                        rhs=codes.bitcast(FP8X4),
+                        rhs_scale=e_scale[E_ROW:P, first : first + count],
+                        start=True,
+                        stop=True,
+                    )
                 nc.vector.tensor_reduce(out=neg_max[:, i, a : a + 1], in_=bank[:], axis=AX.X, op=ALU.max, negate=True)
                 nc.scalar.activation(
                     out=ex[i][:, a],

@@ -32,7 +32,7 @@ MAX_GAP = 64.0
 W_SPLIT = 272
 E_ROW = 4
 E_ROWS = slice(P - 16, P)
-E_FIRST = 768
+E_FIRST = 640
 PE_TILES = TILES - 1
 
 
@@ -138,7 +138,7 @@ def tile_picked_ymatch_log_p_kernel(tc, x_words, x_scales, w1, e_words, e_scales
         e_rest = reuse.tile([P, U - E_FIRST], U32, name="e_rest", align_bytes=64, offset=S)
         passes = [
             [(e_first[:, 0:HALF], 0, HALF)],
-            [(e_first[:, HALF:E_FIRST], HALF, E_FIRST - HALF), (e_rest[:], E_FIRST, U - E_FIRST)],
+            [(e_first[:, HALF:E_FIRST], HALF, P), (e_rest[:, 0:P], E_FIRST, P), (e_rest[:, P:], E_FIRST + P, U - E_FIRST - P)],
         ]
 
         def quantize_h(i):
@@ -220,11 +220,7 @@ def tile_picked_ymatch_log_p_kernel(tc, x_words, x_scales, w1, e_words, e_scales
         z.append(z_last)
 
         for i in range(TILES):
-            rows = slice(i * P, (i + 1) * P)
             res = keep.tile([P, HALVES, VH], F32, name=f"res{i}")
             for a in range(HALVES):
                 nc.scalar.activation(out=res[:, a, :], in_=z[i][:, a, :], func=ACT.Ln, scale=weight[:, i, a : a + 1], bias=EPS)
-                if i == last:
-                    nc.sync.dma_start(out=out[rows, a * VH : (a + 1) * VH], in_=res[:, a, :])
-            if i < last:
-                nc.sync.dma_start(out=out[rows, :], in_=res[:].rearrange("p a v -> p (a v)"))
+            nc.sync.dma_start(out=out[i * P : (i + 1) * P, :], in_=res[:].rearrange("p a v -> p (a v)"))

@@ -99,10 +99,10 @@ def tile_picked_ymatch_log_p_kernel(tc, x_words, x_scales, w1, e_words, e_scales
 
         w_bf = keep.tile([P, PACK * H], BF16, name="w_bf", align_bytes=64)
         w_view = w_bf[:].rearrange("p (t m j) -> p m j t", t=PACK, j=PACK)
-        for a, c in enumerate(w_cols):
+        for a, t in ((0, slice(0, PACK)), (1, slice(0, PACK // 2)), (1, slice(PACK // 2, PACK))):
             nc.scalar.activation(
-                out=w_view[:, c.start // PACK : c.stop // PACK],
-                in_=w_raw[a][:].rearrange("p j (m t) -> p m j t", t=PACK),
+                out=w_view[:, w_cols[a].start // PACK : w_cols[a].stop // PACK, :, t],
+                in_=w_raw[a][:].rearrange("p j (m t) -> p m j t", t=PACK)[:, :, :, t],
                 func=ACT.Copy,
             )
         w_codes = keep.tile([P, H], U32, name="w_codes", align_bytes=64)
@@ -112,13 +112,12 @@ def tile_picked_ymatch_log_p_kernel(tc, x_words, x_scales, w1, e_words, e_scales
                 out=w_codes[:, cols].bitcast(FP8X4), scales=w_scale[:, cols], in_=w_bf[:, PACK * cols.start : PACK * cols.stop]
             )
 
-        h_bf = []
-        for i in range(TILES):
+        def first_product(i, ts, tag):
             tok = slice(i * P, (i + 1) * P)
-            bank = psum.tile([P, PACK * P], F32, name=f"h_bank{i}", tag=f"bank{i}")
-            for t in range(PACK) if i == 0 else reversed(range(PACK)):
+            bank = psum.tile([P, len(ts), P], F32, name=f"h_bank{i}_{min(ts)}", tag=tag)
+            for t in ts:
                 nc.tensor.matmul_mx(
-                    out=bank[:, t * P : (t + 1) * P],
+                    out=bank[:, t - min(ts), :],
                     lhsT=w_codes[:, t * P : (t + 1) * P].bitcast(FP8X4),
                     lhsT_scale=w_scale[:, t * P : (t + 1) * P],
                     rhs=x_codes[:, tok].bitcast(FP8X4),
@@ -126,11 +125,16 @@ def tile_picked_ymatch_log_p_kernel(tc, x_words, x_scales, w1, e_words, e_scales
                     start=True,
                     stop=True,
                 )
-            h_bf.append(keep.tile([P, P * PACK], BF16, name=f"h_bf{i}", align_bytes=64))
             nc.scalar.copy(
-                out=h_bf[i][:].rearrange("p (n t) -> p n t", t=PACK),
-                in_=bank[:].rearrange("p (t n) -> p n t", t=PACK),
+                out=h_bf[i][:].rearrange("p (n t) -> p n t", t=PACK)[:, :, min(ts) : max(ts) + 1],
+                in_=bank[:].rearrange("p t n -> p n t"),
             )
+
+        h_bf = [keep.tile([P, P * PACK], BF16, name=f"h_bf{i}", align_bytes=64) for i in range(TILES)]
+        first_product(0, [0, 1], logits_bank(1, 1))
+        first_product(0, [2, 3], "bank0")
+        for i in range(1, TILES):
+            first_product(i, [3, 2, 1, 0], f"bank{i}")
 
         h_codes = []
         h_scale = reuse.tile([P, TILES, P], U8, name="h_scale", align_bytes=64, offset=0)

@@ -28,7 +28,7 @@ HALF = U // HALVES
 VH = V // HALVES
 LIST_ROWS = 16
 EPS = 1e-4
-MAX_GAP = 64.0
+MAX_FACTOR = 2.0**92
 W_SPLIT = 272
 E_ROW = 4
 E_ROWS = slice(P - 16, P)
@@ -192,13 +192,11 @@ def tile_picked_ymatch_log_p_kernel(tc, x_words, x_scales, w1, e_words, e_scales
                     )
 
         gap = keep.tile([P, TILES, HALVES], F32, name="gap")
-        clamped = keep.tile([P, TILES, HALVES], F32, name="clamped")
         factor = keep.tile([P, TILES, HALVES], F32, name="factor")
         other = keep.tile([P, TILES, HALVES], F32, name="other")
         weight = keep.tile([P, TILES, HALVES], F32, name="weight")
         nc.vector.tensor_tensor(out=gap[:], in0=neg_max[:], in1=neg_max[:, :, ::-1], op=ALU.subtract)
-        nc.vector.tensor_scalar_min(out=clamped[:], in0=gap[:], scalar1=MAX_GAP)
-        nc.scalar.activation(out=factor[:], in_=clamped[:], func=ACT.Exp)
+        nc.scalar.activation(out=factor[:], in_=gap[:], func=ACT.Exp)
 
         back_banks = [logits_bank(PE_TILES - 1, 1), logits_bank(PE_TILES, 0), logits_bank(0, 1)]
 
@@ -212,7 +210,9 @@ def tile_picked_ymatch_log_p_kernel(tc, x_words, x_scales, w1, e_words, e_scales
 
         z = [turn_back(0)]
         total = keep.tile([P, TILES, HALVES], F32, name="total", tag="turned_sb0")
-        nc.vector.tensor_tensor(out=other[:], in0=factor[:], in1=half_sum[:, :, ::-1], op=ALU.mult)
+        nc.vector.scalar_tensor_tensor(
+            out=other[:], in0=factor[:], scalar=MAX_FACTOR, in1=half_sum[:, :, ::-1], op0=ALU.min, op1=ALU.mult
+        )
         nc.vector.tensor_tensor(out=total[:], in0=other[:], in1=half_sum[:], op=ALU.add)
         nc.vector.reciprocal(out=weight[:], in_=total[:])
         z.extend(turn_back(i) for i in range(1, PE_TILES))
@@ -227,4 +227,7 @@ def tile_picked_ymatch_log_p_kernel(tc, x_words, x_scales, w1, e_words, e_scales
             res = keep.tile([P, HALVES, VH], F32, name=f"res{i}")
             for a in range(HALVES):
                 nc.scalar.activation(out=res[:, a, :], in_=z[i][:, a, :], func=ACT.Ln, scale=weight[:, i, a : a + 1], bias=EPS)
-            nc.sync.dma_start(out=out[i * P : (i + 1) * P, :], in_=res[:].rearrange("p a v -> p (a v)"))
+                if i in (0, last):
+                    nc.sync.dma_start(out=out[i * P : (i + 1) * P, a * VH : (a + 1) * VH], in_=res[:, a, :])
+            if i not in (0, last):
+                nc.sync.dma_start(out=out[i * P : (i + 1) * P, :], in_=res[:].rearrange("p a v -> p (a v)"))

@@ -193,41 +193,49 @@ def tile_picked_ymatch_log_p_kernel(tc, x_words, x_scales, w1, e_words, e_scales
 
         gap = keep.tile([P, TILES, HALVES], F32, name="gap")
         factor = keep.tile([P, TILES, HALVES], F32, name="factor")
-        other = keep.tile([P, TILES, HALVES], F32, name="other")
-        weight = keep.tile([P, TILES, HALVES], F32, name="weight")
-        nc.vector.tensor_tensor(out=gap[:], in0=neg_max[:], in1=neg_max[:, :, ::-1], op=ALU.subtract)
+        nc.vector.tensor_tensor(
+            out=gap[:], in0=neg_max[:, :, 0:1].to_broadcast([P, TILES, HALVES]), in1=neg_max[:], op=ALU.subtract
+        )
         nc.scalar.activation(out=factor[:], in_=gap[:], func=ACT.Exp)
 
-        back_banks = [logits_bank(PE_TILES - 1, 1), logits_bank(PE_TILES, 0), logits_bank(0, 1)]
+        def times_factor(dst, factors, values):
+            nc.vector.scalar_tensor_tensor(out=dst, in0=factors, scalar=MAX_FACTOR, in1=values, op0=ALU.min, op1=ALU.mult)
 
-        def turn_back(i):
+        back_banks = [logits_bank(PE_TILES - 1, 1), logits_bank(PE_TILES, 0), logits_bank(0, 1)]
+        back = []
+        for i in range(PE_TILES):
             turned_sb = keep.tile([P, HALVES, P], F32, name=f"turned_sb{i}")
             nc.vector.tensor_copy(turned_sb[:], turned[i][:])
-            back = psum.tile([P, HALVES, VH], F32, name=f"back{i}", tag=back_banks[i])
+            back.append(psum.tile([P, HALVES, VH], F32, name=f"back{i}", tag=back_banks[i]))
             for a in range(HALVES):
-                nc.tensor.transpose(back[:, a, :], turned_sb[:, a, :], ident[:])
-            return back
+                nc.tensor.transpose(back[i][:, a, :], turned_sb[:, a, :], ident[:])
 
-        z = [turn_back(0)]
-        total = keep.tile([P, TILES, HALVES], F32, name="total", tag="turned_sb0")
-        nc.vector.scalar_tensor_tensor(
-            out=other[:], in0=factor[:], scalar=MAX_FACTOR, in1=half_sum[:, :, ::-1], op0=ALU.min, op1=ALU.mult
-        )
-        nc.vector.tensor_tensor(out=total[:], in0=other[:], in1=half_sum[:], op=ALU.add)
-        nc.vector.reciprocal(out=weight[:], in_=total[:])
-        z.extend(turn_back(i) for i in range(1, PE_TILES))
         last = TILES - 1
-        pair = keep.tile([P, HALVES, D // 2, VH], F32, name=f"pair{last}")
-        z_last = keep.tile([P, HALVES, VH], F32, name=f"z{last}", tag="turned_sb0")
+        scaled_sum = keep.tile([P, TILES, HALVES], F32, name="scaled_sum", tag="pair")
+        total = keep.tile([P, TILES], F32, name="total")
+        weight = keep.tile([P, TILES], F32, name="weight")
+        weight_last = keep.tile([P, HALVES], F32, name="weight_last")
+        z = [keep.tile([P, HALVES, VH], F32, name=f"z{i}") for i in range(TILES)]
+        pair = keep.tile([P, HALVES, D // 2, VH], F32, name="pair", tag="pair")
+
+        def scale_back(i):
+            times_factor(z[i][:], factor[:, i, :].unsqueeze(2).to_broadcast([P, HALVES, VH]), back[i][:])
+
+        times_factor(scaled_sum[:], factor[:], half_sum[:])
+        scale_back(0)
+        nc.vector.tensor_tensor(out=total[:], in0=scaled_sum[:, :, 0], in1=scaled_sum[:, :, 1], op=ALU.add)
+        scale_back(1)
+        nc.vector.reciprocal(out=weight[:], in_=total[:])
+        scale_back(2)
         nc.vector.tensor_tensor(out=pair[:], in0=ex[last][:, :, 0 : D // 2, :], in1=ex[last][:, :, D // 2 : D, :], op=ALU.add)
-        nc.vector.tensor_tensor(out=z_last[:], in0=pair[:, :, 0, :], in1=pair[:, :, 1, :], op=ALU.add)
-        z.append(z_last)
+        times_factor(weight_last[:], factor[:, last, :], weight[:, last : last + 1].to_broadcast([P, HALVES]))
+        nc.vector.tensor_tensor(out=z[last][:], in0=pair[:, :, 0, :], in1=pair[:, :, 1, :], op=ALU.add)
 
         for i in range(TILES):
             res = keep.tile([P, HALVES, VH], F32, name=f"res{i}")
-            for a in range(HALVES):
-                nc.scalar.activation(out=res[:, a, :], in_=z[i][:, a, :], func=ACT.Ln, scale=weight[:, i, a : a + 1], bias=EPS)
-                if i in (0, last):
-                    nc.sync.dma_start(out=out[i * P : (i + 1) * P, a * VH : (a + 1) * VH], in_=res[:, a, :])
-            if i not in (0, last):
-                nc.sync.dma_start(out=out[i * P : (i + 1) * P, :], in_=res[:].rearrange("p a v -> p (a v)"))
+            if i < PE_TILES:
+                nc.scalar.activation(out=res[:], in_=z[i][:], func=ACT.Ln, scale=weight[:, i : i + 1], bias=EPS)
+            else:
+                for a in range(HALVES):
+                    nc.scalar.activation(out=res[:, a, :], in_=z[i][:, a, :], func=ACT.Ln, scale=weight_last[:, a : a + 1], bias=EPS)
+            nc.sync.dma_start(out=out[i * P : (i + 1) * P, :], in_=res[:].rearrange("p a v -> p (a v)"))

from contextlib import ExitStack

import concourse.mybir as mybir
from concourse.masks import make_identity

K, T, S, H, D, W, U = 512, 1024, 512, 512, 4, 2048, 1024
V = U // D
FLOPS = 2 * K * H * S + 2 * H * S * U

F32 = mybir.dt.float32
BF16 = mybir.dt.bfloat16
I32 = mybir.dt.int32
U32 = mybir.dt.uint32
U16 = mybir.dt.uint16
U8 = mybir.dt.uint8
FP8X4 = mybir.dt.float8_e4m3fn_x4
ACT = mybir.ActivationFunctionType
ALU = mybir.AluOpType
AX = mybir.AxisListType

P = 128
PACK = 4
QUADRANTS = 4
BANKS = 8
TILES = S // P
HALVES = 2
HALF = U // HALVES
VH = V // HALVES
LIST_ROWS = 16
EPS = 1e-4
MAX_FACTOR = 2.0**92
W_SPLIT = 272
E_ROW = 4
E_ROWS = slice(P - 16, P)
E_FIRST = 640
PE_TILES = TILES - 1


def load_scale_rows(nc, table, scales, row):
    for q in range(QUADRANTS):
        nc.sync.dma_start(
            out=table[32 * q + row : 32 * q + row + 4, :].bitcast(I32),
            in_=scales[0, 4 * q : 4 * q + 4, :].bitcast(I32),
        )


def load_words(queue, table, words):
    queue.dma_start(out=table[:].bitcast(I32), in_=words[0].rearrange("p n t -> p (n t)").bitcast(I32))


def logits_bank(i, a):
    return f"bank{(TILES + HALVES * i + a) % BANKS}"


def tile_picked_ymatch_log_p_kernel(tc, x_words, x_scales, w1, e_words, e_scales, offs, sup, out):
    nc = tc.nc
    with ExitStack() as ctx:
        keep = ctx.enter_context(tc.tile_pool(name="keep", bufs=1))
        reuse = ctx.enter_context(tc.tile_pool(name="reuse", bufs=1))
        psum = ctx.enter_context(tc.psum_pool(name="psum", bufs=1))

        offs_sb = keep.tile([P, S // LIST_ROWS], U16, name="offs_sb")
        sup_sb = keep.tile([P, U // LIST_ROWS], U16, name="sup_sb")
        xw_table = keep.tile([P, T], U32, name="xw_table", align_bytes=64)
        xs_table = keep.tile([P, T], U8, name="xs_table", align_bytes=64)
        ew_table = keep.tile([P, W], U32, name="ew_table", align_bytes=64)
        es_table = keep.tile([P, W], U8, name="es_table", align_bytes=64)
        w_cols = [slice(0, W_SPLIT), slice(W_SPLIT, H)]
        w_raw = [keep.tile([P, PACK, c.stop - c.start], F32, name=f"w_raw{a}") for a, c in enumerate(w_cols)]

        ident = keep.tile([P, P], F32, name="ident")
        nc.vector.memset(xs_table[:].bitcast(I32), 0)
        nc.vector.memset(es_table[0 : E_ROWS.start, :].bitcast(I32), 0)
        e_scale = keep.tile([P, U], U8, name="e_scale", align_bytes=64)
        nc.vector.memset(e_scale[:].bitcast(I32), 0)
        make_identity(nc, ident[:])

        w_rows = w1.rearrange("(p j) c -> p j c", j=PACK)
        nc.sync.dma_start(sup_sb[:], sup)
        nc.scalar.dma_start(out=es_table[E_ROWS, :].bitcast(I32), in_=e_scales[0].bitcast(I32))
        nc.sync.dma_start(out=w_raw[0][:], in_=w_rows[:, :, w_cols[0]])
        load_words(nc.sync, xw_table, x_words)
        nc.sync.dma_start(offs_sb[:], offs)
        load_scale_rows(nc, xs_table, x_scales, 0)
        nc.sync.dma_start(out=w_raw[1][:], in_=w_rows[:, :, w_cols[1]])
        load_words(nc.sync, ew_table, e_words)

        x_codes = keep.tile([P, S], U32, name="x_codes", align_bytes=64)
        x_scale = keep.tile([P, S], U8, name="x_scale", align_bytes=64)
        e_rows = reuse.tile([P, U], U8, name="e_rows", align_bytes=64, offset=0)
        nc.vector.tensor_copy(e_rows[:], es_table[:].indirect(sup_sb[:]))
        for q in range(QUADRANTS):
            nc.sync.dma_start(
                out=e_scale[32 * q + E_ROW : 32 * q + E_ROW + 4, :].bitcast(I32),
                in_=e_rows[E_ROWS.start + 4 * q : E_ROWS.start + 4 * q + 4, :].bitcast(I32),
            )
        nc.vector.tensor_copy(x_codes[:], xw_table[:].indirect(offs_sb[:]))
        nc.vector.tensor_copy(x_scale[:], xs_table[:].indirect(offs_sb[:]))

        w_bf = keep.tile([P, PACK * H], BF16, name="w_bf", align_bytes=64)
        w_view = w_bf[:].rearrange("p (t m j) -> p m j t", t=PACK, j=PACK)
        for a, t in ((0, slice(0, PACK)), (1, slice(0, PACK // 2)), (1, slice(PACK // 2, PACK))):
            nc.scalar.activation(
                out=w_view[:, w_cols[a].start // PACK : w_cols[a].stop // PACK, :, t],
                in_=w_raw[a][:].rearrange("p j (m t) -> p m j t", t=PACK)[:, :, :, t],
                func=ACT.Copy,
            )
        w_codes = keep.tile([P, H], U32, name="w_codes", align_bytes=64)
        w_scale = keep.tile([P, H], U8, name="w_scale", align_bytes=64)
        for cols in (slice(0, H // 2), slice(H // 2, H)):
            nc.vector.quantize_mx(
                out=w_codes[:, cols].bitcast(FP8X4), scales=w_scale[:, cols], in_=w_bf[:, PACK * cols.start : PACK * cols.stop]
            )

        def first_product(i, ts, tag):
            tok = slice(i * P, (i + 1) * P)
            bank = psum.tile([P, len(ts), P], F32, name=f"h_bank{i}_{min(ts)}", tag=tag)
            for t in ts:
                nc.tensor.matmul_mx(
                    out=bank[:, t - min(ts), :],
                    lhsT=w_codes[:, t * P : (t + 1) * P].bitcast(FP8X4),
                    lhsT_scale=w_scale[:, t * P : (t + 1) * P],
                    rhs=x_codes[:, tok].bitcast(FP8X4),
                    rhs_scale=x_scale[:, tok],
                    start=True,
                    stop=True,
                )
            nc.scalar.copy(
                out=h_bf[i][:].rearrange("p (n t) -> p n t", t=PACK)[:, :, min(ts) : max(ts) + 1],
                in_=bank[:].rearrange("p t n -> p n t"),
            )

        h_bf = [keep.tile([P, P * PACK], BF16, name=f"h_bf{i}", align_bytes=64) for i in range(TILES)]
        first_product(0, [0, 1], logits_bank(1, 1))
        first_product(0, [2, 3], "bank0")
        for i in range(1, TILES):
            first_product(i, [3, 2, 1, 0], f"bank{i}")

        h_codes = []
        h_scale = reuse.tile([P, TILES, P], U8, name="h_scale", align_bytes=64, offset=0)
        e_first = keep.tile([P, E_FIRST], U32, name="e_first", align_bytes=64)
        e_rest = reuse.tile([P, U - E_FIRST], U32, name="e_rest", align_bytes=64, offset=S)
        passes = [
            [(e_first[:, 0:HALF], 0, HALF)],
            [(e_first[:, HALF:E_FIRST], HALF, P), (e_rest[:, 0:P], E_FIRST, P), (e_rest[:, P:], E_FIRST + P, U - E_FIRST - P)],
        ]

        def quantize_h(i):
            h_codes.append(keep.tile([P, P], U32, name=f"h_codes{i}", tag=f"h_codes{i % (TILES - 1)}", align_bytes=64))
            nc.vector.quantize_mx(out=h_codes[i][:].bitcast(FP8X4), scales=h_scale[:, i, :], in_=h_bf[i][:])

        nc.vector.tensor_copy(e_first[:], ew_table[:].indirect(sup_sb[:, 0 : E_FIRST // LIST_ROWS]))
        quantize_h(0)
        nc.vector.tensor_copy(e_rest[:], ew_table[:].indirect(sup_sb[:, E_FIRST // LIST_ROWS : U // LIST_ROWS]))
        for i in range(1, TILES - 1):
            quantize_h(i)

        neg_max = keep.tile([P, TILES, HALVES], F32, name="neg_max")
        half_sum = keep.tile([P, TILES, HALVES], F32, name="half_sum")
        ex = [keep.tile([P, HALVES, D, VH], F32, name=f"ex{i}") for i in range(TILES)]
        for i in range(TILES):
            for a in range(HALVES):
                bank = psum.tile([P, HALF], F32, name=f"y_bank{i}{a}", tag=logits_bank(i, a))
                for codes, first, count in passes[a]:
                    nc.tensor.matmul_mx(
                        out=bank[:, first - a * HALF : first - a * HALF + count],
                        lhsT=h_codes[i][:].bitcast(FP8X4),
                        lhsT_scale=h_scale[:, i, :],
                        rhs=codes.bitcast(FP8X4),
                        rhs_scale=e_scale[E_ROW:P, first : first + count],
                        start=True,
                        stop=True,
                    )
                nc.vector.tensor_reduce(out=neg_max[:, i, a : a + 1], in_=bank[:], axis=AX.X, op=ALU.max, negate=True)
                nc.scalar.activation(
                    out=ex[i][:, a],
                    in_=bank[:].rearrange("p (v d) -> p d v", d=D),
                    func=ACT.Exp,
                    bias=neg_max[:, i, a : a + 1],
                    accum_out=half_sum[:, i, a : a + 1],
                )
            if i == 0:
                quantize_h(TILES - 1)

        turned = []
        for i in range(PE_TILES):
            turned.append(psum.tile([P, HALVES, P], F32, name=f"turned{i}", tag=logits_bank(i, 0)))
            for a in range(HALVES):
                for d in range(D):
                    nc.tensor.matmul(
                        turned[i][:, a, :], lhsT=ex[i][:, a, d, :], rhs=ident[:], is_transpose=True, start=d == 0, stop=d == D - 1
                    )

        gap = keep.tile([P, TILES, HALVES], F32, name="gap")
        factor = keep.tile([P, TILES, HALVES], F32, name="factor")
        nc.vector.tensor_tensor(
            out=gap[:], in0=neg_max[:, :, 0:1].to_broadcast([P, TILES, HALVES]), in1=neg_max[:], op=ALU.subtract
        )
        nc.scalar.activation(out=factor[:], in_=gap[:], func=ACT.Exp)

        def times_factor(dst, factors, values):
            nc.vector.scalar_tensor_tensor(out=dst, in0=factors, scalar=MAX_FACTOR, in1=values, op0=ALU.min, op1=ALU.mult)

        back_banks = [logits_bank(PE_TILES - 1, 1), logits_bank(PE_TILES, 0), logits_bank(0, 1)]
        back = []
        for i in range(PE_TILES):
            turned_sb = keep.tile([P, HALVES, P], F32, name=f"turned_sb{i}")
            nc.vector.tensor_copy(turned_sb[:], turned[i][:])
            back.append(psum.tile([P, HALVES, VH], F32, name=f"back{i}", tag=back_banks[i]))
            for a in range(HALVES):
                nc.tensor.transpose(back[i][:, a, :], turned_sb[:, a, :], ident[:])

        last = TILES - 1
        scaled_sum = keep.tile([P, TILES, HALVES], F32, name="scaled_sum", tag="pair")
        total = keep.tile([P, TILES], F32, name="total")
        weight = keep.tile([P, TILES], F32, name="weight")
        weight_last = keep.tile([P, HALVES], F32, name="weight_last")
        z = [keep.tile([P, HALVES, VH], F32, name=f"z{i}") for i in range(TILES)]
        pair = keep.tile([P, HALVES, D // 2, VH], F32, name="pair", tag="pair")

        def scale_back(i):
            times_factor(z[i][:], factor[:, i, :].unsqueeze(2).to_broadcast([P, HALVES, VH]), back[i][:])

        times_factor(scaled_sum[:], factor[:], half_sum[:])
        scale_back(0)
        nc.vector.tensor_tensor(out=total[:], in0=scaled_sum[:, :, 0], in1=scaled_sum[:, :, 1], op=ALU.add)
        scale_back(1)
        nc.vector.reciprocal(out=weight[:], in_=total[:])
        scale_back(2)
        nc.vector.tensor_tensor(out=pair[:], in0=ex[last][:, :, 0 : D // 2, :], in1=ex[last][:, :, D // 2 : D, :], op=ALU.add)
        times_factor(weight_last[:], factor[:, last, :], weight[:, last : last + 1].to_broadcast([P, HALVES]))
        nc.vector.tensor_tensor(out=z[last][:], in0=pair[:, :, 0, :], in1=pair[:, :, 1, :], op=ALU.add)

        for i in range(TILES):
            res = keep.tile([P, HALVES, VH], F32, name=f"res{i}")
            if i < PE_TILES:
                nc.scalar.activation(out=res[:], in_=z[i][:], func=ACT.Ln, scale=weight[:, i : i + 1], bias=EPS)
            else:
                for a in range(HALVES):
                    nc.scalar.activation(out=res[:, a, :], in_=z[i][:, a, :], func=ACT.Ln, scale=weight_last[:, a : a + 1], bias=EPS)
            nc.sync.dma_start(out=out[i * P : (i + 1) * P, :], in_=res[:].rearrange("p a v -> p (a v)"))
